import numpy as np, ml_dtypes
CORES = [16,18,20,22]
N = 4
BF = ml_dtypes.bfloat16
def gentries(a):
    return np.ascontiguousarray(a.reshape(8, 16, -1).transpose(0, 2, 1)).reshape(8, -1)
def gtable(e):
    e = np.asarray(e); return np.ascontiguousarray(e.reshape(8, -1, 16).transpose(0, 2, 1)).reshape(128, -1).astype(np.int32)
M, D, L, Q = 4096, 4, 4, 2048
S = [0, 4096, 6144, 7168, 7680, 7936]
NODES = S[-1]; FULL = 2 ** L - 1; QP = Q // N
def gtables(a):
    return np.stack([gtable(e) for e in a])
def letters(rng, *shape):
    return np.left_shift(np.uint8(1), rng.integers(0, L, shape, dtype=np.uint8))
def anyset(rng, *shape):
    return rng.integers(1, FULL + 1, shape, dtype=np.uint8)
def tobf(v):
    return v.astype(np.float32).astype(BF)
def pairs(rng):
    le = np.zeros((N, 8, NODES - M), np.int64); ri = le.copy()
    for d in range(1, D + 1):
        e = S[d - 1] + np.argsort(rng.random((N, 8, S[d] - S[d - 1])), axis=2); a, b = S[d] - M, S[d + 1] - M
        le[:, :, a:b] = e[:, :, 0::2]; ri[:, :, a:b] = e[:, :, 1::2]
    return le, ri
def nodes(rng):
    d = rng.integers(0, D + 1, (N, 8, Q)); lo = np.array(S)[d]; n = np.array(S)[d + 1] - lo
    return lo + np.minimum((rng.random((N, 8, Q)) * n).astype(np.int64), n - 1)
def setup_inputs(rng):
    le, ri = pairs(rng)
    leaf = np.where(rng.random((N, 128, M), dtype=np.float32) < 0.125, anyset(rng, N, 128, M), letters(rng, N, 128, M))
    return {"leaf": tobf(leaf), "left": gtables(le), "right": gtables(ri), "clade": gtables(nodes(rng)), "edge": gtables(nodes(rng))}
def setup_inputs_near(rng):
    d = setup_inputs(rng); rate = np.repeat(0.1 * (1 + np.arange(8)), 16).reshape(1, 128, 1).astype(np.float32)
    leaf = np.where(rng.random((N, 128, M), dtype=np.float32) < rate, d["leaf"].astype(np.float32), letters(rng, 1, 128, 1).astype(np.float32))
    d["leaf"] = tobf(leaf); return d
def setup_inputs_order(rng):
    d = setup_inputs(rng); le = np.zeros((N, 8, NODES - M), np.int64); ri = le.copy()
    for k in range(1, D + 1):
        e = np.arange(S[k - 1], S[k]); a, b = S[k] - M, S[k + 1] - M
        le[0::2, :, a:b] = e[0::2]; ri[0::2, :, a:b] = e[1::2]
        le[1::2, :, a:b] = e[::-1][0::2]; ri[1::2, :, a:b] = e[::-1][1::2]
    d["left"] = gtables(le); d["right"] = gtables(ri)
    j = np.broadcast_to(np.arange(Q), (N, 8, Q))
    d["edge"] = gtables(j); d["clade"] = gtables(NODES - 1 - j); return d
def setup_inputs_few(rng):
    d = setup_inputs(rng); p = np.array([0, M - 1, M, S[D], NODES - 1])
    d["clade"] = gtables(p[rng.integers(0, 5, (N, 8, Q))]); d["edge"] = gtables(p[rng.integers(0, 5, (N, 8, Q))]); return d
def setup_inputs_far(rng):
    d = setup_inputs_order(rng); h = M // 2
    a = rng.integers(0, L, (1, 128, 1)); b = (a + rng.integers(1, L, (1, 128, 1))) % L
    leaf = np.where(np.arange(M) < h, np.left_shift(1, a), np.left_shift(1, b))
    d["leaf"] = tobf(np.repeat(leaf, N, axis=0))
    c = rng.integers(h, M, (N, 8, Q)); mv = (rng.random((N, 8, Q)) < 0.125) & (np.arange(8).reshape(1, 8, 1) >= 4)
    d["clade"] = gtables(np.where(mv, c - h, c)); d["edge"] = gtables(rng.integers(0, h, (N, 8, Q))); return d
def setup_inputs_spread(rng):
    d = setup_inputs(rng); p = rng.random((N, 128, L)) ** 3 + 1e-6; c = np.add.accumulate(p, axis=2); c = (c / c[:, :, -1:]).astype(np.float32)
    x = rng.random((N, 128, M), dtype=np.float32); lt = np.zeros((N, 128, M), np.uint8)
    for k in range(L - 1): lt += x > c[:, :, k:k + 1]
    am = rng.choice(np.array([0, 0, 0, 0.02, 0.02, 1], np.float32), (N, 1, M))
    amb = np.where(rng.random((N, 128, M), dtype=np.float32) < 0.5, np.uint8(FULL), anyset(rng, N, 128, M))
    d["leaf"] = tobf(np.where(rng.random((N, 128, M), dtype=np.float32) < am, amb, np.left_shift(np.uint8(1), lt)))
    e = np.minimum((NODES * rng.random((N, 8, Q)) ** 4).astype(np.int64), NODES - 1); h = np.minimum((NODES * rng.random((N, 8, Q)) ** 4).astype(np.int64), NODES - 1)
    d["edge"] = gtables(e); d["clade"] = gtables(NODES - 1 - h); return d
def check_inputs(d):
    bad = []
    try:
        v = d["leaf"].astype(np.float32)
        if not ((v == np.floor(v)) & (v >= 1) & (v <= FULL)).all(): bad.append("leaf")
        ok = True
        for q in range(N):
            le, ri = gentries(d["left"][q]), gentries(d["right"][q])
            for k in range(1, D + 1):
                a, b = S[k] - M, S[k + 1] - M
                e = np.sort(np.concatenate([le[:, a:b], ri[:, a:b]], axis=1), axis=1)
                ok = ok and bool((e == np.arange(S[k - 1], S[k])).all())
        if not ok: bad.append("left and right")
        for a in ("clade", "edge"):
            if not ((d[a] >= 0) & (d[a] < NODES)).all(): bad.append(a)
    except Exception:
        bad.append("shapes")
    return bad
def fitch(a, b):
    i = a & b
    return np.where(i > 0, i, a | b)
def reference(leaf, left, right, clade, edge):
    inside = np.zeros((N, 8, 16, NODES), np.uint8); outside = np.full((N, 8, 16, NODES), FULL, np.uint8)
    inside[:, :, :, :M] = leaf.astype(np.float32).astype(np.uint8).reshape(N, 8, 16, M)
    for q in range(N):
        le, ri = gentries(left[q]), gentries(right[q])
        for g in range(8):
            u, o = inside[q, g], outside[q, g]
            for d in range(1, D + 1):
                x, z = le[g, S[d] - M:S[d + 1] - M], ri[g, S[d] - M:S[d + 1] - M]
                u[:, S[d]:S[d + 1]] = fitch(u[:, x], u[:, z])
            for d in range(D, 0, -1):
                x, z = le[g, S[d] - M:S[d + 1] - M], ri[g, S[d] - M:S[d + 1] - M]
                o[:, x] = fitch(o[:, S[d]:S[d + 1]], u[:, z])
                o[:, z] = fitch(o[:, S[d]:S[d + 1]], u[:, x])
    on = fitch(inside, outside); c = np.zeros((N, 8, Q), np.int64)
    for r in range(N):
        cl, ed = gentries(clade[r]), gentries(edge[r])
        for g in range(8):
            for q in range(N):
                j = slice(q * QP, (q + 1) * QP)
                c[r, g, j] = np.sum((inside[q, g][:, cl[g, j]] & on[r, g][:, ed[g, j]]) == 0, axis=0)
    runs = c.reshape(N, 8, 8, Q // 8)
    return {"cost": np.min(runs, axis=2).astype(np.float32), "first": np.argmin(runs, axis=2).astype(np.float32)}

@@ -1,0 +1,453 @@
+from concourse.bass import DstId, RemoteDMATransfer
+from concourse.mybir import AluOpType as OP, ActivationFunctionType as AF
+
+S = [0, 4096, 6144, 7168, 7680, 7936]
+NT = 12
+PB = 14
+CHUNK = {1: 512, 2: 256, 3: 256, 4: 256}
+GA, SC = 1.56, 3.8
+LATE = 12000
+BY_A = ((1, 0),)
+BY_V = (0, 1024)
+BY_MAX = (1024, 1536)
+BY_REL = (0,)
+CONV_A = (512, 1024, 1536, 3072)
+ON_V = (("r", 0), ("r", 1024), ("r", 2048), ("r", 3072), ("r", 3328), ("r", 3584))
+
+BUFS = {
+    "bfloat16": {"raw": 4096, "f2": 2048, "f4": 2048, "f8": 2048, "win": 7936, "X": 5888, "Y": 4112, "ca": 1792, "cb": 1792,
+                 "oo": 1024, "tY": 256 * NT, "tB": 256 * NT, "uh": 256 * NT, "ul": 256 * NT,
+                 "ole": 2048, "ye": 2048, "ine": 2048, "zz": 2048, "land": 2048, "clout": 2048, "one": 512, "gsum": 192,
+                 "ku": 128, "kc": 128, "kd": 128, "ke": 128, "kmat": 256, "inv": 64},
+    "float32": {"key": 512, "res": 128, "W": 7936, "val": 4096, "ek": 128, "el": 128, "onef": 128, "i1f": 128, "selm": 2048},
+    "int32": {"tS": 256 * NT, "tT": 256 * NT, "li": 240, "ri": 240, "ci": 128, "ei": 128, "keyi": 192},
+    "uint16": {"lo": 240, "ro": 240, "cu": 128, "cin": 128, "eu": 128, "e1": 128, "e2": 128},
+}
+DIAG = {"i1": 1.0, "i2": 2.0, "i8": 8.0, "i32": 32.0, "ik": -256.0, "ip": 2.0 ** -PB, "iq": 2.0 ** PB}
+SCRATCH = {}
+for _t in BUFS:
+    for _b in BUFS[_t]:
+        SCRATCH[_b] = ("sbuf", [32 if _b in ("key", "keyi", "res") else 128, BUFS[_t][_b]], _t)
+for _b in DIAG:
+    SCRATCH[_b] = ("sbuf", [128, 128], "bfloat16")
+for _b in range(8):
+    SCRATCH["ps%d" % _b] = ("psum", [128, 512], "float32")
+SEMAPHORES = (["qV", "qA", "qP", "qG", "snd"] + ["ld%d" % i for i in range(10)] + ["lst%d" % i for i in range(4)]
+              + ["clr%d" % i for i in range(4)])
+
+
+def rank_program(g, core, T, topo):
+    rank = T.rank_of(core)
+    if rank is None:
+        return
+    others = [q for q in range(len(T.cores)) if q != rank]
+    ops = []
+
+    def op(eng, fns, cost, R=(), W=(), lat=0.0, dma=None, inc=0, seen=None):
+        ops.append({"eng": eng, "fns": fns, "cost": cost, "R": list(R), "W": list(W), "lat": lat, "dma": dma, "inc": inc, "seen": seen})
+
+    def V(fn, n, c, R, W):
+        op("V", [fn], 30 + 1.04 * max(64, n * c), R, W)
+
+    def A(fn, n, c, R, W):
+        op("A", [fn], 50 + 1.04 * n * c, R, W)
+
+    def P(fns, n, R, W):
+        op("P", fns, 20 + 0.45 * max(64, n) * len(fns), R, W)
+
+    def G(fn, n, R, W):
+        op("G", [fn], 150 + 2.08 * n, R, W)
+
+    on = lambda k, a: "V" if (k, a) in ON_V else "A"
+    bank, slots = [0], [0]
+
+    def newbank():
+        bank[0] += 1
+        return "ps%d" % ((bank[0] - 1) % 8)
+
+    def newslot(n):
+        a = slots[0] if slots[0] % (256 * NT) + n <= 256 * NT else slots[0] + 256
+        slots[0] = a + n
+        return a % (256 * NT)
+
+    def reg(b, a, n):
+        return (b, 0, 512) if b[:2] == "ps" else (b, a, a + n)
+
+    def mm(ps, terms, n, start=True, stop=True):
+        fns = []
+        for k, (m, b, a) in enumerate(terms):
+            st, sp = start and k == 0, stop and k == len(terms) - 1
+            fns.append(lambda m=m, b=b, a=a, st=st, sp=sp: g.tensor.matmul(T[ps][:, 0:n], T[m][:], T[b][:, a:a + n], st, sp))
+        P(fns, n, [(m, 0, 128) for m, b, a in terms] + [(b, a, a + n) for m, b, a in terms], [(ps, 0, 512)])
+
+    def ts(dst, d0, src, s0, n, c, s1=None, op0=None, s2=None, op1=None):
+        o, i = (lambda: T[dst][:, d0:d0 + n]), (lambda: T[src][:, s0:s0 + n])
+        if op0 is None:
+            fn = lambda: g.vector.tensor_copy(o(), i())
+        elif op1 is None:
+            fn = lambda: g.vector.tensor_scalar(o(), i(), s1, None, op0)
+        else:
+            fn = lambda: g.vector.tensor_scalar(o(), i(), s1, s2, op0, op1)
+        V(fn, n, c, [reg(src, s0, n)], [reg(dst, d0, n)])
+
+    def tt(dst, d0, x, x0, y, y0, n, c, o):
+        V(lambda: g.vector.tensor_tensor(T[dst][:, d0:d0 + n], T[x][:, x0:x0 + n], T[y][:, y0:y0 + n], o), n, c,
+          [reg(x, x0, n), reg(y, y0, n)], [reg(dst, d0, n)])
+
+    def act(dst, d0, src, s0, n, func=AF.Copy, scale=1.0, bias=0.0):
+        A(lambda: g.scalar.activation(T[dst][:, d0:d0 + n], T[src][:, s0:s0 + n], func, bias=bias, scale=scale), n, 1,
+          [reg(src, s0, n)], [reg(dst, d0, n)])
+
+    def fill(buf, p0, p1, a, b, x):
+        V(lambda: g.vector.memset(T[buf][p0:p1, a:b], x), b - a, .5, [], [(buf, a, b)])
+
+    def split(lo, hi, n, kind, z=None):
+        pp, o = newbank(), newslot(max(n, 256))
+        mm(pp, [("i1", b, a) for b, a in hi] + [("ip", b, a) for b, a in lo], n)
+        if kind in ("edge", "out"):
+            ts("tS", o, pp, 0, n, 1, 2.0 ** PB, OP.mult, float((256 << PB) + 256), OP.add)
+        else:
+            ts("tS", o, pp, 0, n, 1, 2.0 ** PB, OP.mult)
+        ts("tT", o, "tS", o, n, 1, 1, OP.logical_shift_right, (0x55 if kind == "test" else 0xD5) + (0xD5 << PB), OP.bitwise_and)
+        ts("tY", o, "tT", o, n, 1, 2.0 ** -PB, OP.mult, *((-256.0, OP.add) if kind == "out" else ()))
+        mm(pp, [("iq", "tY", o)] + ([("kc", "one", 0)] if kind == "out" else []), n)
+        if kind == "test":
+            tt("zz", z, "tT", o, pp, 0, n, 1, OP.is_equal)
+        else:
+            tt("tB", o, "tT", o, pp, 0, n, 1, OP.subtract)
+        return o
+
+    def pair(lo, hi, n, kind, const, his, los):
+        o, ph = split(lo, hi, n, kind), newbank()
+        mm(ph, [("i1", b, a) for b, a in hi] + ([(const, "one", 0)] if his else []), n, stop=False)
+        pl = newbank()
+        mm(pl, [("i1", b, a) for b, a in lo] + ([(const, "one", 0)] if los else []), n, stop=False)
+        mm(ph, [("ik", "tY", o)], n, start=False)
+        mm(pl, [("ik", "tB", o)], n, start=False)
+        return ph, pl, o
+
+    KC = {"in": "ku", "edge": "ke", "out": "kd"}
+
+    def double(lo, hi, n, kind, dh, h0, dl, l0):
+        ph, pl, o = pair(lo, hi, n, kind, KC[kind], True, True)
+        h0, l0 = (o if h0 is None else h0), (o if l0 is None else l0)
+        tt(dh, h0, "tY", o, ph, 0, n, 1, OP.max)
+        tt(dl, l0, "tB", o, pl, 0, n, 1, OP.max)
+        return o
+
+    def double_a(lo, hi, n, kind, dh, h0, dl, l0):
+        ph, pl, o = pair(lo, hi, n, kind, KC[kind], True, False)
+        tt(dh, h0, "tY", o, ph, 0, n, 1, OP.max)
+        act("ul", o, pl, 0, n, AF.Relu, 1.0, (-128 if kind == "out" else 128) * 256.0)
+        pf = newbank()
+        mm(pf, [("i1", "tB", o), ("i1", "ul", o)], n)
+        act(dl, l0, pf, 0, n)
+
+    def gather(eng, dst, d0, src, a, b, off, c0, n, bias=0.0):
+        ind = lambda: T[src][:, a:b].indirect(T[off][:, c0:c0 + n // 16])
+        R, W = [(src, a, b), (off, c0, c0 + n // 16)], [(dst, d0, d0 + n)]
+        if eng == "V" and bias:
+            V(lambda: g.vector.tensor_scalar(T[dst][:, d0:d0 + n], ind(), bias, None, OP.add), n, GA, R, W)
+        elif eng == "V":
+            V(lambda: g.vector.tensor_copy(T[dst][:, d0:d0 + n], ind()), n, GA, R, W)
+        else:
+            A(lambda: g.scalar.activation(T[dst][:, d0:d0 + n], ind(), AF.Copy, bias=bias), n, GA, R, W)
+
+    def silu(win, a, b, off, c0, src, s0, n):
+        A(lambda: g.scalar.activation(T[win][:, a:b].indirect(T[off][:, c0:c0 + n // 16]), T[src][:, s0:s0 + n], AF.Silu), n, SC,
+          [(src, s0, s0 + n), (off, c0, c0 + n // 16)], [(win, a, b)])
+        ops[-1]["late"] = LATE
+
+    CA = lambda c: ("Y", 2048 + c) if c < 2048 else ("ca", c - 2048)
+    CB = lambda c: ("Y", c) if c < 2048 else ("cb", c - 2048)
+    OO = lambda c: ("X", c) if c < 2048 else ("oo", c - 2048) if c < 3072 else ("X", S[3] - 2048 + c - 3072)
+
+    def load(eng, i, dst, a, b, src, lat):
+        q = g.sync if eng == "Y" else g.scalar
+        op(eng, [lambda: q.dma_start(T[dst][:, a:b], T[src][:, a:b])], 120, [], [(dst, a, b)], lat=lat, dma="ld%d" % i, inc=16)
+
+    for k in range(4):
+        load("Y", k, "raw", 1024 * k, 1024 * k + 1024, "leaf", 2000 + 800 * k)
+    load("A", 4, "ci", 0, 128, "clade", 2200)
+    load("A", 5, "li", 0, 240, "left", 2600)
+    load("A", 6, "ri", 0, 240, "right", 3000)
+    load("Y", 7, "ei", 0, 128, "edge", 6500)
+
+    fill("one", 0, 128, 0, 512, 1.0)
+    G(lambda: g.affine_select(T.i1[:], T.one[:, 0:128], [[-1, 128]], OP.is_equal, 0.0, 0, 1), 128, [("one", 0, 128)], [("i1", 0, 128)])
+    for nm in DIAG:
+        if nm != "i1":
+            ts(nm, 0, "i1", 0, 128, .5, DIAG[nm], OP.mult)
+    fill("ku", 0, 128, 0, 128, 255.0)
+    fill("kc", 0, 64, 0, 128, 2.0 ** (PB + 2))
+    fill("kc", 64, 128, 0, 128, 4.0)
+    fill("kd", 0, 64, 0, 128, -512.0)
+    fill("kd", 64, 128, 0, 128, -2.0)
+    fill("ke", 0, 64, 0, 128, 512.0)
+    fill("ke", 64, 128, 0, 128, 2.0)
+    fill("onef", 0, 128, 0, 128, 1.0)
+    fill("inv", 0, 128, 0, 64, 2.0 ** -7)
+
+    ts("cu", 0, "ci", 0, 128, 1)
+    for d in range(1, 5):
+        c0, c1 = (S[d] - 4096) // 16, (S[d + 1] - 4096) // 16
+        for x, y in (("li", "lo"), ("ri", "ro")):
+            ts(y, c0, x, c0, c1 - c0, 1, float(-S[d - 1]), OP.add)
+
+    def fused(src, dst, w, sem):
+        tr = []
+        for i, q in enumerate(others):
+            to = T.cores[q]
+            rid, pid, _e = topo.addr(to)
+            en = topo.engines(core, to)[4 * i:4 * i + 4]
+            tr.append(RemoteDMATransfer(dst_ids=[DstId(rid=rid, pnc=pid)], dma_engine_mask=sum(1 << e for e in en),
+                                        remote_sem=T.sem[sem + str(rank)], src=T[src][:, w * q:w * q + w],
+                                        dst=T[dst][:, w * rank:w * rank + w]))
+        g.remote_dma_fused(tr, local_sem=T.sem.snd)
+        return None
+
+    def exchange(src, dst, w, sem, t):
+        op("G", [lambda: fused(src, dst, w, sem)], 1500, [(src, w * q, w * q + w) for q in others], [], lat=2000, dma="snd", inc=12)
+        for q in others:
+            op(None, [], t, [], [(dst, w * q, w * q + w)], seen=(sem + str(q), 4))
+
+    exchange("cu", "cin", 32, "lst", 6000)
+    ts("eu", 0, "ei", 0, 128, 1)
+
+    for a in range(0, 4096, 512):
+        f = a % 2048
+        ts("f2", f, "raw", a, 512, .5, .5, OP.mult, 132 - .25, OP.add)
+        ts("f4", f, "raw", a, 512, .5, .25, OP.mult, 131 - .375, OP.add)
+        ps, terms = newbank(), [("i2", "f2", f), ("i8", "f4", f), ("i32", "f8", f)]
+        if a not in CONV_A:
+            ts("f8", f, "raw", a, 512, .5, 8.0, OP.is_ge, -37.0, OP.add)
+            mm(ps, terms, 512)
+            tt("win", a, "raw", a, ps, 0, 512, 1, OP.add)
+        else:
+            act("f8", f, "raw", a, 512, AF.Copy, .125, 129 - .4375)
+            mm(ps, [("i1", "raw", a)] + terms, 512)
+            act("win", a, ps, 0, 512, AF.Copy, 1.0, 128.0 - 32.0 * (129 + 41))
+
+    def ramp(buf, a, n, step, base):
+        G(lambda: g.iota(T[buf][:, a:a + n], [[step, n]], base, 0, allow_small_or_imprecise_dtypes=True), n, [("i1", 0, 128)], [(buf, a, a + n)])
+
+    V(lambda: g.vector.memset(T.X[:, S[4] - 2048:S[5] - 2048], 85.0), 256, .5, [], [("X", S[4] - 2048, S[5] - 2048)])
+    for a in range(0, 4096, 512):
+        ramp("val", a, 512, 1, 4096 + a)
+    ramp("Y", 4096, 16, 0, 256)
+    for a in range(4096, S[5], 1280):
+        ramp("W", a, 1280, 1, 4096 + a)
+    G(lambda: g.affine_select(T.i1f[:], T.onef[:], [[-1, 128]], OP.is_equal, 0.0, 0, 1), 128, [("onef", 0, 128)], [("i1f", 0, 128)])
+    for s in range(16):
+        G(lambda s=s: g.affine_select(T.selm[:, 128 * s:128 * s + 128], T.i1f[:], [[0, 8], [1, 16]], OP.is_equal, 0.0, -s, 0), 128,
+          [("i1f", 0, 128)], [("selm", 128 * s, 128 * s + 128)])
+    G(lambda: g.iota(T.kmat[:], [[1, 8], [0, 32]], 0, 0, allow_small_or_imprecise_dtypes=True), 256, [], [("kmat", 0, 256)])
+
+    for a in range(0, 2048, 256):
+        silu("W", 0, 4096, "lo", a // 16, "val", a, 256)
+        silu("W", 0, 4096, "ro", a // 16, "val", 2048 + a, 256)
+
+    for d in range(1, 5):
+        base, nn, n = S[d] - 4096, S[d + 1] - S[d], CHUNK[d]
+        for a in range(0, nn, n):
+            c, w, h = base + a, S[d] + a, n // 2
+            bias = -128.0 if d > 2 else 0.0
+            gather(on("l", c), *CA(c), "win", S[d - 1], S[d], "lo", c // 16, n, bias)
+            gather(on("r", c), *CB(c), "win", S[d - 1], S[d], "ro", c // 16, n, bias)
+            double([CA(c), CB(c)], [CA(c + h), CB(c + h)], h, "edge" if d > 2 else "in", "win", w + h, "win", w)
+
+    for x, y in (("cb", "lo"), ("ca", "ro")):
+        V(lambda x=x, y=y: g.vector.tensor_copy(T.X[:, S[3] - 2048:S[4] - 2048].indirect(T[y][:, 224:240]), T[x][:, 1536:1792]), 256, SC,
+          [(x, 1536, 1792), (y, 224, 240)], [("X", S[3] - 2048, S[4] - 2048)])
+
+    for q in others + [rank]:
+        dst, off = ("land", "cu") if q == rank else ("clout", "cin")
+        gather("A", dst, 512 * q, "win", 0, S[5], off, 32 * q, 512)
+    exchange("clout", "land", 512, "clr", 35000)
+
+    for a in range(0, 2048, 512):
+        gather("A", "val", a, "W", 0, S[5], "eu", a // 16, 512)
+    ps = newbank()
+    for s in range(16):
+        P([lambda s=s, ps=ps: g.tensor.matmul(T[ps][:, 0:128], T.selm[:, 128 * s:128 * s + 128], T.val[:, s:2048:16], s == 0, s == 15)],
+          512, [("selm", 128 * s, 128 * s + 128), ("val", 0, 2048)], [(ps, 0, 512)])
+    ts("e2", 0, ps, 0, 128, 1, -4095.75, OP.add, 4096.25, OP.min)
+    ts("ek", 0, ps, 0, 128, 1, 6143.5, OP.is_ge, -2048.0, OP.mult)
+    tt("el", 0, "ek", 0, ps, 0, 128, 1, OP.add)
+    ts("e1", 0, "el", 0, 128, 1, -4095.75, OP.add)
+
+    for d in (3, 2, 1):
+        base, nn, n, h = S[d] - 4096, S[d + 1] - S[d], *((1024, 512) if d == 1 else (512, 256))
+        lo_, hi_ = S[d - 1] - 2048, S[d] - 2048
+        for a in range(0, nn, n):
+            c, w = base + a, S[d] + a - 2048
+            if d < 3:
+                (double_a if (d, a) in BY_A else double)([("X", w)], [("X", w + h)], h, "out" if d == 2 else "edge", *OO(c + h), *OO(c))
+            if d > 1:
+                q = c - 2048
+                ob, oa = OO(c)
+                for off, sib in (("lo", "cb"), ("ro", "ca")):
+                    V(lambda off=off, sib=sib, c=c, q=q, n=n, lo_=lo_, hi_=hi_, ob=ob, oa=oa: g.vector.tensor_tensor(
+                        T.X[:, lo_:hi_].indirect(T[off][:, c // 16:(c + n) // 16]), T[ob][:, oa:oa + n], T[sib][:, q:q + n], OP.add), n, SC,
+                      [(ob, oa, oa + n), (sib, q, q + n), (off, c // 16, (c + n) // 16)], [("X", lo_, hi_)])
+
+    def sel(d0, s0, src, pat, o, base, cm):
+        G(lambda: g.affine_select(T.gsum[:, d0:d0 + 32], T[src][:, s0:s0 + 32], pat, o, 0.0, base, cm), 32, [reg(src, s0, 32)], [("gsum", d0, d0 + 32)])
+
+    sel(128, 0, "one", [[-16, 8], [0, 4]], OP.is_ge, 0, 1)
+    sel(160, 128, "gsum", [[16, 8], [0, 4]], OP.is_ge, 15, -1)
+    ts("gsum", 128, "gsum", 160, 32, 1, 8.0, OP.mult)
+    for b in range(4):
+        sel(32 * b, 128, "gsum", [[0, 8], [1, 4]], OP.is_equal, -b, 0)
+
+    blocks, n, mid, mid2 = range(0, 2048, 512), 256, {}, {}
+    for a in blocks:
+        gather("A", "ine", a, "win", 0, S[5], "eu", a // 16, 512)
+    for a in blocks:
+        gather("A", "ye", a, "Y", 0, 4112, "e2", a // 16, 512, -256.0)
+    for a in blocks:
+        if a in BY_V:
+            V(lambda a=a: g.vector.tensor_tensor(T.ole[:, a:a + 512], T.X[:, 0:S[5] - 2048].indirect(T.e1[:, a // 16:a // 16 + 32]), T.ye[:, a:a + 512], OP.add), 512, GA,
+              [("X", 0, S[5] - 2048), ("e1", a // 16, a // 16 + 32), ("ye", a, a + 512)], [("ole", a, a + 512)])
+        else:
+            gather("A", "ole", a, "X", 0, S[5] - 2048, "e1", a // 16, 512)
+    for a in blocks:
+        sum_ = lambda x: [("ole", x)] + ([] if a in BY_V else [("ye", x)])
+        if a in BY_MAX:
+            o = double(sum_(a), sum_(a + n), n, "edge", "uh", None, "ul", None)
+        else:
+            ph, pl, o = pair(sum_(a), sum_(a + n), n, "edge", "ke", a not in BY_REL, False)
+            if a in BY_REL:
+                act("uh", o, ph, 0, n, AF.Relu, 1.0, 128 * 256.0)
+            else:
+                tt("uh", o, "tY", o, ph, 0, n, 1, OP.max)
+            act("ul", o, pl, 0, n, AF.Relu, 1.0, 128 * 256.0)
+        mid[a] = o
+    for a in blocks:
+        h, o = a + n, mid[a]
+        tl = [] if a in BY_MAX else [("tB", o)]
+        th = [("tY", o)] if a in BY_REL else []
+        ph, pl, o2 = pair([("ine", a), ("ul", o)] + tl, [("ine", h), ("uh", o)] + th, n, "in", "ku", False, False)
+        act("uh", o2, ph, 0, n, AF.Relu, 1.0, 127 * 256.0)
+        act("ul", o2, pl, 0, n, AF.Relu, 1.0, 127 * 256.0)
+        mid2[a] = o2
+    for a in blocks:
+        h, o2 = a + n, mid2[a]
+        o = split([("land", a), ("tB", o2), ("ul", o2)], [("land", h), ("uh", o2), ("tY", o2)], n, "test", a)
+        act("zz", h, "tY", o, n, AF.Relu, -1.0, 129.0)
+        ps = newbank()
+        fns = []
+        for kk in range(2):
+            k = a // 256 + kk
+            for b in range(4):
+                fns.append(lambda kk=kk, b=b, ps=ps, a=a: g.tensor.matmul(
+                    T[ps][0:32, 64 * kk:64 * kk + 64], T.gsum[:, 32 * b:32 * b + 32],
+                    T.zz[:, a + 256 * kk + 64 * b:a + 256 * kk + 64 * b + 64], b == 0, False))
+            fns.append(lambda kk=kk, k=k, ps=ps: g.tensor.matmul(
+                T[ps][0:32, 64 * kk:64 * kk + 64], T.kmat[:, 32 * k:32 * k + 32], T.inv[:], False, True))
+        P(fns, 64, [("gsum", 0, 128), ("zz", a, a + 512), ("kmat", 0, 256), ("inv", 0, 64)], [(ps, 0, 512)])
+        r = a // 4
+        if a == 0:
+            A(lambda ps=ps: g.scalar.activation(T.key[:, 0:128], T[ps][0:32, 0:128], AF.Copy), 128, 1, [(ps, 0, 512)], [("key", 0, 128)])
+        else:
+            V(lambda ps=ps, r=r: g.vector.tensor_tensor(T.key[:, r:r + 128], T.key[:, r - 128:r], T[ps][0:32, 0:128], OP.min), 128, 1,
+              [(ps, 0, 512), ("key", r - 128, r)], [("key", r, r + 128)])
+    tt("keyi", 0, "key", 384, "key", 448, 64, 2, OP.min)
+    ts("keyi", 64, "keyi", 0, 64, 1, 3, OP.logical_shift_right)
+    ts("keyi", 128, "keyi", 0, 64, 1, 7, OP.bitwise_and)
+    ts("res", 0, "keyi", 64, 64, 1)
+    ts("res", 64, "keyi", 128, 64, 1)
+    op("Y", [lambda: g.sync.dma_start(T.cost[:], T.res[:, 0:64])], 120, [("res", 0, 64)], [], lat=2000, dma="ld8", inc=16)
+    op("A", [lambda: g.scalar.dma_start(T["first"][:], T.res[:, 64:128])], 120, [("res", 64, 128)], [], lat=2000, dma="ld9", inc=16)
+
+    run(g, T, ops)
+
+
+def run(g, T, ops):
+    n = len(ops)
+    deps = [dict() for _ in ops]
+    hist = {}
+    for i, o in enumerate(ops):
+        for kind, regs in (("R", o["R"]), ("W", o["W"])):
+            for r in regs:
+                psum = r[0][:2] == "ps"
+                for (a, b, j, w) in hist.get(r[0], ()):
+                    if j == i or not (a < r[2] and r[1] < b):
+                        continue
+                    same = ops[j]["eng"] == o["eng"]
+                    if not w and kind == "R" and (same or not psum):
+                        continue
+                    hard = (w and kind == "R") or not same or ops[j]["dma"] is not None or o["eng"] != "P"
+                    deps[i][j] = deps[i].get(j, False) or hard
+        for r in o["R"]:
+            hist.setdefault(r[0], []).append((r[1], r[2], i, False))
+        for r in o["W"]:
+            h = hist.get(r[0], [])
+            hist[r[0]] = [e for e in h if not (r[1] <= e[0] and e[1] <= r[2])] + [(r[1], r[2], i, True)]
+    succ = [[] for _ in ops]
+    for i in range(n):
+        for j in deps[i]:
+            succ[j].append(i)
+    tail = [0.0] * n
+    for i in range(n - 1, -1, -1):
+        tail[i] = ops[i]["cost"] + ops[i]["lat"] + max([tail[k] + 80 for k in succ[i]] or [0.0])
+    for i in range(n):
+        tail[i] -= ops[i].get("late", 0)
+    free, fin = {}, [0.0] * n
+    need = [len(d) for d in deps]
+    ready = [i for i in range(n) if not need[i]]
+    est = dict((i, 0.0) for i in ready)
+    order = []
+    while ready:
+        best = min(ready, key=lambda i: max(est[i], free.get(ops[i]["eng"], 0.0) if ops[i]["eng"] else 0.0))
+        e = ops[best]["eng"]
+        bt = max(est[best], free.get(e, 0.0) if e else 0.0)
+        if e:
+            cand = [i for i in ready if ops[i]["eng"] == e and max(est[i], free.get(e, 0.0)) <= bt + 60]
+            best = max(cand, key=lambda i: (tail[i], -i))
+            bt = max(est[best], free.get(e, 0.0))
+            free[e] = bt + ops[best]["cost"]
+        fin[best] = bt + ops[best]["cost"] + ops[best]["lat"]
+        order.append(best)
+        ready.remove(best)
+        for k in succ[best]:
+            need[k] -= 1
+            if not need[k]:
+                ready.append(k)
+                est[k] = max(fin[j] + 80 for j in deps[k])
+    queue = {"V": g.vector, "A": g.scalar, "P": g.tensor, "G": g, "Y": g.sync}
+    csem = {"V": "qV", "A": "qA", "P": "qP", "G": "qG"}
+    total, val = {}, [None] * n
+    clock = {e: {} for e in queue}
+    snap = [None] * n
+    for i in order:
+        o = ops[i]
+        e = o["eng"]
+        if e is None:
+            val[i], snap[i] = o["seen"], {}
+            total[o["seen"][0]] = o["seen"][1]
+            continue
+        ck = clock[e]
+        todo = sorted([j for j in deps[i] if deps[i][j]], key=lambda j: -fin[j])
+        for j in todo:
+            s = val[j][0]
+            if ck.get(s, 0) >= val[j][1]:
+                continue
+            same = [x for x in todo if val[x][0] == s]
+            v = max(val[x][1] for x in same)
+            queue[e].wait_ge(T.sem[s], v)
+            for x in same:
+                for k2, v2 in snap[x].items():
+                    ck[k2] = max(ck.get(k2, 0), v2)
+            ck[s] = max(ck.get(s, 0), v)
+        s = o["dma"] or csem[e]
+        for fn in o["fns"]:
+            ins = fn()
+            if ins is not None:
+                ins.then_inc(T.sem[s], o["inc"] or 1)
+            total[s] = total.get(s, 0) + (o["inc"] or 1)
+        val[i], snap[i] = (s, total[s]), dict(ck)
+    for s in sorted(total):
+        if clock["Y"].get(s, 0) < total[s]:
+            g.sync.wait_ge(T.sem[s], total[s])
+    return fin

@@ -2,28 +2,61 @@ from concourse.bass import DstId, RemoteDMATransfer
 from concourse.mybir import AluOpType as OP, ActivationFunctionType as AF
 
 S = [0, 4096, 6144, 7168, 7680, 7936]
-NT = 12
-PB = 14
-CHUNK = {1: 512, 2: 256, 3: 256, 4: 256}
-GA, SC = 1.56, 3.8
-LATE = 12000
-BY_A = ((1, 0),)
-BY_V = (0, 1024)
-BY_MAX = (1024, 1536)
-BY_REL = (0,)
-CONV_A = (512, 1024, 1536, 3072)
-ON_V = (("r", 0), ("r", 1024), ("r", 2048), ("r", 3072), ("r", 3328), ("r", 3584))
+NT = 24
+PB = 16
+K = {
+    "CHUNK": {1: 512, 2: 512, 3: 256, 4: 256},
+    "DOWN": {3: 512, 2: 512, 1: 512},
+    "GA": 1.56, "SC": 3.8, "PE": .45,
+    "LATE": 0,
+    "WCH": 256,
+    "UP_A": (),
+    "BY_A": (0, 512, 1024, 1536),
+    "BY_V": (0, 1024),
+    "EV1": (512, 1536),
+    "EV2": (0, 512, 1024, 1536),
+    "CONT": True,
+    "CONV_A": (512, 1536, 2560, 3584),
+    "F8_A": (),
+    "ON_V": (("r", 0), ("r", 1024), ("r", 2048), ("r", 3072), ("r", 3328), ("r", 3584)),
+    "LOADS": (("Y", "leaf", 0), ("A", "left", 0), ("A", "right", 0), ("Y", "leaf", 1), ("Y", "leaf", 2), ("Y", "leaf", 3), ("A", "clade", 0), ("Y", "edge", 0)),
+    "T0": 2000, "DT": 500, "WIN": 60, "HOP": 80, "KEEP": 3, "LOOK": 2, "URG": 3000, "FR": .6, "SK": (1, 1, 4), "ROUNDS": 5, "CUT": 0, "TOP": 20000,
+}
+K.update(SK=(.5, .5, 3), ON_V=(("r", 0), ("r", 2048), ("r", 2304), ("r", 2560), ("r", 3072), ("r", 3328), ("r", 3584)),
+         CHUNK={1: 512, 2: 256, 3: 256, 4: 256}, LATE=15000, FR=.8, DOWN={3: 256, 2: 256, 1: 512}, KEEP=2, TOP=3000, UP_A=(0, 3584), BY_A=(0, 512, 1024), BY_V=(0, 1536),
+         CONV_A=(0, 512, 1536, 2560, 3072))
+K.update(HOP=150, PE=.38, T0=1600, DT=400, GA=1.45, SC=3.6, WAW=True, EARLY=3000, UP_1=(), DN_1=(), URG=1500, DOWN={3: 512, 2: 256, 1: 512})
+K.update(WAW=True, UP_A=(0, 512, 1024, 2048, 3584), DN_1=((2, 0), (1, 1536)), BY_V=(0, 1024), HOP=160,
+         ON_V=(("r", 0), ("r", 1024), ("r", 2048), ("r", 2304), ("r", 2560), ("r", 3072), ("r", 3328), ("r", 3584)))
+K.update(WLR=(256, 256), E1=0, E2=0, DN_1=(), DOWN={3: 512, 2: 256, 1: 512})
+K.update(UP_A=(3584,), LATE=0, EARLY=30000, WLR=(256, 512),
+         ON_V=tuple(("r", a) for a in (0, 512, 1024, 2048, 2304, 2560, 2816, 3072, 3328, 3584)) + tuple(("s", a) for a in (0, 512, 1024, 1536)) + (("w", 0), ("w", 512)))
+K.update(DEEP=4, G1=0, E0=3, E2=3, MORE=300, TOL=0, UP=100, PARTS=(512, 512, 512, 256, 256))
+K.update(ROB=.5, OWN=110, CONV_P=(), PARTS=(512,) * 4, PE=.31, SC=3.2, GA=1.4, MORE=0, HOP=150, DOWN={3: 512, 2: 512, 1: 512}, CONV_A=(0, 512, 1024, 1536, 2048, 2560),
+         ON_V=tuple(("r", a) for a in (0, 1024, 2048, 2304, 2560, 3072, 3328, 3584)) + tuple(("s", a) for a in (0, 512, 1024, 1536)) + (("w", 0), ("w", 512)))
+K.update(MORE=300, ON_V=K["ON_V"] + (("r", 512), ("r", 2816)))
+K.update(FIX=(48, 68), FIRST=45000, BACK=6000)
+K.update(E0=0, E2=0, MORE=0, ROB=0, HOP=160, OWN=160, PE=.38, GA=1.45, SC=3.6, FIX=(35, 50, 50), DOWN={3: 512, 2: 256, 1: 512}, CONV_A=(0, 512, 1536, 2560, 3072))
+K.update(FIX=(30, 195, 72), PE=.355, GA=1.56, SC=3.8, HOP=90, OWN=70, ROB=.5, DOWN={3: 512, 2: 512, 1: 512}, E2=3, UP_A=())
+K.update(MORE=100, CONV_A=(0, 1536, 2560), ON_V=tuple(("r", a) for a in (0, 1024, 2048, 2304, 2560, 3072, 3328, 3584))
+         + (("X", 4096), ("X", 4608), ("X", 2560), ("X", 3584), ("u3", 0)) + tuple(("s", a) for a in (0, 512, 1024, 1536)))
+K.update(MORE=0, HOP=200, OWN=180, FIX=(25, 160, 70), PE=.33, GA=1.4, SC=3.2)
+K.update(E2=0, E0=3, CONV_A=(0, 512, 1536, 2560, 3072), ON_V=tuple(("r", a) for a in (0, 512, 1024, 2048, 2304, 2560, 2816, 3072, 3328, 3584))
+         + tuple(("s", a) for a in (0, 512, 1024, 1536)) + (("w", 0), ("w", 512)))
+K.update(TURN=3500, BY_V=(0,), MORE=100, ON_V=K["ON_V"] + tuple(("X", 2048 + a) for a in (0, 1024, 512, 1536)))
+K.update(WLR=(512, 512), MORE=250, ROB=1, E2=3)
+PLAN = {}
 
 BUFS = {
-    "bfloat16": {"raw": 4096, "f2": 2048, "f4": 2048, "f8": 2048, "win": 7936, "X": 5888, "Y": 4112, "ca": 1792, "cb": 1792,
-                 "oo": 1024, "tY": 256 * NT, "tB": 256 * NT, "uh": 256 * NT, "ul": 256 * NT,
-                 "ole": 2048, "ye": 2048, "ine": 2048, "zz": 2048, "land": 2048, "clout": 2048, "one": 512, "gsum": 192,
-                 "ku": 128, "kc": 128, "kd": 128, "ke": 128, "kmat": 256, "inv": 64},
-    "float32": {"key": 512, "res": 128, "W": 7936, "val": 4096, "ek": 128, "el": 128, "onef": 128, "i1f": 128, "selm": 2048},
-    "int32": {"tS": 256 * NT, "tT": 256 * NT, "li": 240, "ri": 240, "ci": 128, "ei": 128, "keyi": 192},
-    "uint16": {"lo": 240, "ro": 240, "cu": 128, "cin": 128, "eu": 128, "e1": 128, "e2": 128},
+    "bfloat16": {"raw": 4096, "f2": 2048, "f8": 2048, "win": 7936, "X": 7936, "eight": 32, "Y": 6144, "ca": 1792, "cb": 1792,
+                 "u3": 512, "tt": 512 * NT, "s1": 2048, "s2": 2048,
+                 "ole": 2048, "ine": 2048, "zz": 2048, "land": 2048, "clout": 2048, "one": 512, "gsum": 192,
+                 "ke": 128, "kmat": 256, "inv": 64},
+    "float32": {"key": 512, "res": 128, "W": 7936, "val": 2048, "ek": 256, "el": 128, "onef": 128, "i1f": 128, "ef": 128},
+    "int32": {"ej": 128, "tS": 256 * NT, "tT": 256 * NT, "li": 480, "ci": 256, "keyi": 192},
+    "uint16": {"lr": 480, "cu": 256, "cin": 128, "e1": 128, "ev": 128},
 }
-DIAG = {"i1": 1.0, "i2": 2.0, "i8": 8.0, "i32": 32.0, "ik": -256.0, "ip": 2.0 ** -PB, "iq": 2.0 ** PB}
+DIAG = {"i1": 1.0, "m1": -1.0, "mq": -2.0 ** PB, "i2": 2.0, "i8": 8.0, "i32": 32.0, "ik": -256.0, "iq": 2.0 ** PB, "ip": 2.0 ** -PB, "i14": 2.0 ** 14, "kn": -2.0 ** 33, "kp": 2.0 ** 33}
 SCRATCH = {}
 for _t in BUFS:
     for _b in BUFS[_t]:
@@ -31,8 +64,8 @@ for _t in BUFS:
 for _b in DIAG:
     SCRATCH[_b] = ("sbuf", [128, 128], "bfloat16")
 for _b in range(8):
-    SCRATCH["ps%d" % _b] = ("psum", [128, 512], "float32")
-SEMAPHORES = (["qV", "qA", "qP", "qG", "snd"] + ["ld%d" % i for i in range(10)] + ["lst%d" % i for i in range(4)]
+    SCRATCH["pb%d" % _b] = ("psum", [128, 512], "float32")
+SEMAPHORES = (["qV", "qA", "qP", "qG", "snd", "acc", "ac2", "dup"] + ["ld%d" % i for i in range(12)] + ["lst%d" % i for i in range(4)]
               + ["clr%d" % i for i in range(4)])
 
 
@@ -41,29 +74,37 @@ def rank_program(g, core, T, topo):
     if rank is None:
         return
     others = [q for q in range(len(T.cores)) if q != rank]
-    ops = []
+    gate = [None]
+    ops, hold, skew = [], {}, [0]
+    B = dict((b, T[b]) for b in SCRATCH)
+    GA, SC = K["GA"], K["SC"]
+    RANGE = ({GA: 1.95, SC: 5.3}, {GA: 1.1, SC: 1.9})
 
     def op(eng, fns, cost, R=(), W=(), lat=0.0, dma=None, inc=0, seen=None):
-        ops.append({"eng": eng, "fns": fns, "cost": cost, "R": list(R), "W": list(W), "lat": lat, "dma": dma, "inc": inc, "seen": seen})
+        ops.append({"eng": eng, "fns": fns, "cost": cost, "R": list(R), "W": list(W), "lat": lat, "dma": dma, "inc": inc, "seen": seen,
+                    "late": skew[0]})
 
     def V(fn, n, c, R, W):
-        op("V", [fn], 30 + 1.04 * max(64, n * c), R, W)
+        op("V", [fn], K["FIX"][0] + .83 * max(64, n * c), R, W)
+        ops[-1]["more"] = [.83 * n * (x.get(c, c) - c) for x in RANGE]
 
     def A(fn, n, c, R, W):
-        op("A", [fn], 50 + 1.04 * n * c, R, W)
+        op("A", [fn], K["FIX"][1 if c == 1 else 2] + .83 * n * c, R, W)
+        ops[-1]["more"] = [.83 * n * (x.get(c, c) - c) for x in RANGE]
 
     def P(fns, n, R, W):
-        op("P", fns, 20 + 0.45 * max(64, n) * len(fns), R, W)
+        op("P", fns, 8 + (6 + K["PE"] * max(64, n)) * len(fns), R, W)
 
     def G(fn, n, R, W):
-        op("G", [fn], 150 + 2.08 * n, R, W)
+        op("G", [fn], 150 + 1.66 * n, R, W)
 
-    on = lambda k, a: "V" if (k, a) in ON_V else "A"
+    on = lambda k, a: "V" if (k, a) in K["ON_V"] else "A"
     bank, slots = [0], [0]
 
-    def newbank():
+    def newbank(held=False):
         bank[0] += 1
-        return "ps%d" % ((bank[0] - 1) % 8)
+        hold["ps%d" % bank[0]] = (0, K["KEEP"], K["DEEP"])[held]
+        return "ps%d" % bank[0]
 
     def newslot(n):
         a = slots[0] if slots[0] % (256 * NT) + n <= 256 * NT else slots[0] + 256
@@ -77,11 +118,11 @@ def rank_program(g, core, T, topo):
         fns = []
         for k, (m, b, a) in enumerate(terms):
             st, sp = start and k == 0, stop and k == len(terms) - 1
-            fns.append(lambda m=m, b=b, a=a, st=st, sp=sp: g.tensor.matmul(T[ps][:, 0:n], T[m][:], T[b][:, a:a + n], st, sp))
+            fns.append(lambda m=m, b=b, a=a, st=st, sp=sp: g.tensor.matmul(B[ps][:, 0:n], T[m][:, 0:128], T[b][:, a:a + n], st, sp))
         P(fns, n, [(m, 0, 128) for m, b, a in terms] + [(b, a, a + n) for m, b, a in terms], [(ps, 0, 512)])
 
     def ts(dst, d0, src, s0, n, c, s1=None, op0=None, s2=None, op1=None):
-        o, i = (lambda: T[dst][:, d0:d0 + n]), (lambda: T[src][:, s0:s0 + n])
+        o, i = (lambda: B[dst][:, d0:d0 + n]), (lambda: B[src][:, s0:s0 + n])
         if op0 is None:
             fn = lambda: g.vector.tensor_copy(o(), i())
         elif op1 is None:
@@ -91,57 +132,89 @@ def rank_program(g, core, T, topo):
         V(fn, n, c, [reg(src, s0, n)], [reg(dst, d0, n)])
 
     def tt(dst, d0, x, x0, y, y0, n, c, o):
-        V(lambda: g.vector.tensor_tensor(T[dst][:, d0:d0 + n], T[x][:, x0:x0 + n], T[y][:, y0:y0 + n], o), n, c,
+        V(lambda: g.vector.tensor_tensor(B[dst][:, d0:d0 + n], B[x][:, x0:x0 + n], B[y][:, y0:y0 + n], o), n, c,
           [reg(x, x0, n), reg(y, y0, n)], [reg(dst, d0, n)])
 
     def act(dst, d0, src, s0, n, func=AF.Copy, scale=1.0, bias=0.0):
-        A(lambda: g.scalar.activation(T[dst][:, d0:d0 + n], T[src][:, s0:s0 + n], func, bias=bias, scale=scale), n, 1,
+        A(lambda: g.scalar.activation(B[dst][:, d0:d0 + n], B[src][:, s0:s0 + n], func, bias=bias, scale=scale), n, 1,
           [reg(src, s0, n)], [reg(dst, d0, n)])
+
+    def out(dst, d0, ps, n, bias=0.0):
+        if on(dst, d0) == "V":
+            ts(dst, d0, ps, 0, n, 1, *((bias, OP.add) if bias else ()))
+        else:
+            act(dst, d0, ps, 0, n, AF.Copy, 1.0, bias)
 
     def fill(buf, p0, p1, a, b, x):
         V(lambda: g.vector.memset(T[buf][p0:p1, a:b], x), b - a, .5, [], [(buf, a, b)])
 
-    def split(lo, hi, n, kind, z=None):
-        pp, o = newbank(), newslot(max(n, 256))
-        mm(pp, [("i1", b, a) for b, a in hi] + [("ip", b, a) for b, a in lo], n)
-        if kind in ("edge", "out"):
-            ts("tS", o, pp, 0, n, 1, 2.0 ** PB, OP.mult, float((256 << PB) + 256), OP.add)
+    HIGH = {"i1": "iq", "m1": "mq"}
+
+    def split(terms, n, kind, add=None, z=None, short=0, early=0):
+        pp, o, pb = newbank(2 * (early & 1) if add is None else 1), newslot(max(n, 256)), 14 if kind == "edge" else PB
+        both = [x for m, b, a in terms for x in (("i14" if kind == "edge" else HIGH[m], b, a + n), (m, b, a))]
+        if add is not None:
+            mm(pp, both[:1], n, stop=False)
+            both = [("kn", "tt", 2 * add + n), ("kp", "tt", 2 * add + n), both[1], ("kn", "tt", 2 * add), ("kp", "tt", 2 * add)] + both[2:]
+        if early & 1:
+            mm(pp, both[:2], n, stop=False)
+            ops[-1]["after"] = gate[0]
+        mm(pp, both[2 * (early & 1):], n, start=not early & 1 and add is None)
+        short += 256 if kind == "edge" else 0
+        if add is not None:
+            tt("tS", o, "tT", add, pp, 0, n, 1, OP.add)
         else:
-            ts("tS", o, pp, 0, n, 1, 2.0 ** PB, OP.mult)
-        ts("tT", o, "tS", o, n, 1, 1, OP.logical_shift_right, (0x55 if kind == "test" else 0xD5) + (0xD5 << PB), OP.bitwise_and)
-        ts("tY", o, "tT", o, n, 1, 2.0 ** -PB, OP.mult, *((-256.0, OP.add) if kind == "out" else ()))
-        mm(pp, [("iq", "tY", o)] + ([("kc", "one", 0)] if kind == "out" else []), n)
+            ts("tS", o, pp, 0, n, 1, *((float((short << pb) + short), OP.add) if short else ()))
+        top = 0xD5 if kind == "edge" else 0x55
+        ts("tT", o, "tS", o, n, 1, 1, OP.logical_shift_right, top + (top << pb), OP.bitwise_and)
+        if kind == "edge":
+            ts("tt", 2 * o + n, "tT", o, n, 1, 2.0 ** -pb, OP.mult)
+        else:
+            ts("tt", 2 * o + n, "tT", o, n, 1, 1.5 * 2.0 ** (23 + pb), OP.add, 1.5 * 2.0 ** (23 + pb), OP.subtract)
+        mm(pp, [("i14" if kind == "edge" else "i1", "tt", 2 * o + n)], n)
         if kind == "test":
             tt("zz", z, "tT", o, pp, 0, n, 1, OP.is_equal)
         else:
-            tt("tB", o, "tT", o, pp, 0, n, 1, OP.subtract)
+            tt("tt", 2 * o, "tT", o, pp, 0, n, 1, OP.subtract)
         return o
 
-    def pair(lo, hi, n, kind, const, his, los):
-        o, ph = split(lo, hi, n, kind), newbank()
-        mm(ph, [("i1", b, a) for b, a in hi] + ([(const, "one", 0)] if his else []), n, stop=False)
-        pl = newbank()
-        mm(pl, [("i1", b, a) for b, a in lo] + ([(const, "one", 0)] if los else []), n, stop=False)
-        mm(ph, [("ik", "tY", o)], n, start=False)
-        mm(pl, [("ik", "tB", o)], n, start=False)
-        return ph, pl, o
+    def absorb(ps, o, n, more=(), stop=True):
+        mm(ps, [("kn", "tt", 2 * o), ("kp", "tt", 2 * o)] + [("i1", b, a) for b, a in more], 2 * n, start=False, stop=False)
+        P([lambda: g.tensor.matmul(B[ps][:, 0:n], T.i1[:], T.tt[:, 2 * o:2 * o + n], False, False),
+           lambda: g.tensor.matmul(B[ps][:, n:2 * n], T.ip[:], T.tt[:, 2 * o + n:2 * o + 2 * n], False, stop)], n,
+          [("i1", 0, 128), ("ip", 0, 128), ("tt", 2 * o, 2 * o + 2 * n)], [(ps, 0, 512)])
 
-    KC = {"in": "ku", "edge": "ke", "out": "kd"}
+    def double(terms, n, dst, d0, by_a, bias=128.0, more=(), short=0, early=0):
+        o, ps = split(terms, n, "pure" if by_a else "edge", short=short, early=early), newbank(2 if early & 2 else 1)
+        terms = ([("one", "one", 0)] if short else []) + ([] if by_a else [("ke", "one", 0)]) + terms
+        if early & 2:
+            mm(ps, terms[:-1], 2 * n, stop=False)
+            ops[-1]["after"] = gate[0]
+        mm(ps, terms[-1:] if early & 2 else terms, 2 * n, start=not early & 2, stop=False)
+        if by_a:
+            if more and on(dst, d0) == "V":
+                absorb(ps, o, n, more[1:])
+                tt(dst, d0, *more[0], ps, 0, 2 * n, 1, OP.add)
+            else:
+                absorb(ps, o, n, more)
+                out(dst, d0, ps, 2 * n, bias)
+        else:
+            mm(ps, [("ik", "tt", 2 * o)], 2 * n, start=False)
+            tt(dst, d0, "tt", 2 * o, ps, 0, 2 * n, 1, OP.max)
 
-    def double(lo, hi, n, kind, dh, h0, dl, l0):
-        ph, pl, o = pair(lo, hi, n, kind, KC[kind], True, True)
-        h0, l0 = (o if h0 is None else h0), (o if l0 is None else l0)
-        tt(dh, h0, "tY", o, ph, 0, n, 1, OP.max)
-        tt(dl, l0, "tB", o, pl, 0, n, 1, OP.max)
-        return o
-
-    def double_a(lo, hi, n, kind, dh, h0, dl, l0):
-        ph, pl, o = pair(lo, hi, n, kind, KC[kind], True, False)
-        tt(dh, h0, "tY", o, ph, 0, n, 1, OP.max)
-        act("ul", o, pl, 0, n, AF.Relu, 1.0, (-128 if kind == "out" else 128) * 256.0)
-        pf = newbank()
-        mm(pf, [("i1", "tB", o), ("i1", "ul", o)], n)
-        act(dl, l0, pf, 0, n)
+    def single(terms, n, dst, d0, by_a, bias=128.0, more=(), short=0, early=0):
+        pp, o, ps, n = newbank(), newslot(max(2 * n, 256)), newbank(True), 2 * n
+        mm(pp, terms, n)
+        ts("tS", o, pp, 0, n, 1, *((float(short), OP.add) if short else ()))
+        ts("tT", o, "tS", o, n, 1, 1, OP.logical_shift_right, 0x55, OP.bitwise_and)
+        ts("tt", 2 * o, "tT", o, n, 1, *(() if by_a else (128.0, OP.add)))
+        mm(ps, terms + ([("one", "one", 0)] if short else []) + ([] if by_a else [("ke", "one", 0)]), n, stop=False)
+        if by_a:
+            mm(ps, [(m, "tt", 2 * o) for m in ("kn", "kp", "i1")] + [("i1", b, a) for b, a in more], n, start=False)
+            act(dst, d0, ps, 0, n, AF.Copy, 1.0, bias)
+        else:
+            mm(ps, [("ik", "tt", 2 * o)], n, start=False)
+            tt(dst, d0, "tt", 2 * o, ps, 0, n, 1, OP.max)
 
     def gather(eng, dst, d0, src, a, b, off, c0, n, bias=0.0):
         ind = lambda: T[src][:, a:b].indirect(T[off][:, c0:c0 + n // 16])
@@ -153,46 +226,40 @@ def rank_program(g, core, T, topo):
         else:
             A(lambda: g.scalar.activation(T[dst][:, d0:d0 + n], ind(), AF.Copy, bias=bias), n, GA, R, W)
 
-    def silu(win, a, b, off, c0, src, s0, n):
-        A(lambda: g.scalar.activation(T[win][:, a:b].indirect(T[off][:, c0:c0 + n // 16]), T[src][:, s0:s0 + n], AF.Silu), n, SC,
-          [(src, s0, s0 + n), (off, c0, c0 + n // 16)], [(win, a, b)])
-        ops[-1]["late"] = LATE
+    def silu(eng, b, c0, src, s0, n):
+        to, R = (lambda: T.W[:, 0:b].indirect(T.lr[:, c0:c0 + n // 16])), [(src, s0, s0 + n), ("lr", c0, c0 + n // 16)]
+        if eng == "V":
+            V(lambda: g.vector.tensor_copy(to(), T[src][:, s0:s0 + n]), n, SC, R, [("W", 0, b)])
+        else:
+            A(lambda: g.scalar.activation(to(), T[src][:, s0:s0 + n], AF.Silu), n, SC, R, [("W", 0, b)])
+        ops[-1]["late"] = K["LATE"]
 
     CA = lambda c: ("Y", 2048 + c) if c < 2048 else ("ca", c - 2048)
-    CB = lambda c: ("Y", c) if c < 2048 else ("cb", c - 2048)
-    OO = lambda c: ("X", c) if c < 2048 else ("oo", c - 2048) if c < 3072 else ("X", S[3] - 2048 + c - 3072)
+    CB = lambda c: ("Y", 4096 + c) if c < 2048 else ("cb", c - 2048)
 
-    def load(eng, i, dst, a, b, src, lat):
-        q = g.sync if eng == "Y" else g.scalar
-        op(eng, [lambda: q.dma_start(T[dst][:, a:b], T[src][:, a:b])], 120, [], [(dst, a, b)], lat=lat, dma="ld%d" % i, inc=16)
-
-    for k in range(4):
-        load("Y", k, "raw", 1024 * k, 1024 * k + 1024, "leaf", 2000 + 800 * k)
-    load("A", 4, "ci", 0, 128, "clade", 2200)
-    load("A", 5, "li", 0, 240, "left", 2600)
-    load("A", 6, "ri", 0, 240, "right", 3000)
-    load("Y", 7, "ei", 0, 128, "edge", 6500)
+    SRC = {"leaf": ("raw", 1024, 0), "left": ("li", 240, 0), "right": ("li", 240, 240), "clade": ("ci", 128, 0), "edge": ("ci", 128, 128)}
+    for i, (eng, src, k) in enumerate(K["LOADS"]):
+        dst, w, d0 = SRC[src]
+        q, d0 = g.sync if eng == "Y" else g.scalar, d0 + k * w
+        op(eng, [lambda q=q, dst=dst, src=src, a=k * w, w=w, d0=d0: q.dma_start(T[dst][:, d0:d0 + w], T[src][:, a:a + w])], 100, [], [(dst, d0, d0 + w)],
+           lat=K["T0"] + K["DT"] * i + {"clade": 1500, "edge": 6000}.get(src, 0), dma="ld%d" % i, inc=16)
+        ops[-1]["late"] = -1e6 + 1e4 * i
 
     fill("one", 0, 128, 0, 512, 1.0)
     G(lambda: g.affine_select(T.i1[:], T.one[:, 0:128], [[-1, 128]], OP.is_equal, 0.0, 0, 1), 128, [("one", 0, 128)], [("i1", 0, 128)])
     for nm in DIAG:
         if nm != "i1":
             ts(nm, 0, "i1", 0, 128, .5, DIAG[nm], OP.mult)
-    fill("ku", 0, 128, 0, 128, 255.0)
-    fill("kc", 0, 64, 0, 128, 2.0 ** (PB + 2))
-    fill("kc", 64, 128, 0, 128, 4.0)
-    fill("kd", 0, 64, 0, 128, -512.0)
-    fill("kd", 64, 128, 0, 128, -2.0)
     fill("ke", 0, 64, 0, 128, 512.0)
     fill("ke", 64, 128, 0, 128, 2.0)
     fill("onef", 0, 128, 0, 128, 1.0)
     fill("inv", 0, 128, 0, 64, 2.0 ** -7)
 
+    ts("cu", 128, "ci", 128, 128, 1)
+    skew[0] = -K["EARLY"]
+    ts("lr", 0, "li", 0, 480, 1)
+    skew[0] = -K["FIRST"]
     ts("cu", 0, "ci", 0, 128, 1)
-    for d in range(1, 5):
-        c0, c1 = (S[d] - 4096) // 16, (S[d + 1] - 4096) // 16
-        for x, y in (("li", "lo"), ("ri", "ro")):
-            ts(y, c0, x, c0, c1 - c0, 1, float(-S[d - 1]), OP.add)
 
     def fused(src, dst, w, sem):
         tr = []
@@ -208,166 +275,182 @@ def rank_program(g, core, T, topo):
 
     def exchange(src, dst, w, sem, t):
         op("G", [lambda: fused(src, dst, w, sem)], 1500, [(src, w * q, w * q + w) for q in others], [], lat=2000, dma="snd", inc=12)
+        me = len(ops) - 1
         for q in others:
             op(None, [], t, [], [(dst, w * q, w * q + w)], seen=(sem + str(q), 4))
+            ops[-1]["after"] = me
 
-    exchange("cu", "cin", 32, "lst", 6000)
-    ts("eu", 0, "ei", 0, 128, 1)
+    exchange("cu", "cin", 32, "lst", 9000)
+    skew[0] = 0
 
     for a in range(0, 4096, 512):
         f = a % 2048
+        ts("Y", f, "raw", a, 512, .5, .25, OP.mult, 131 - .375, OP.add)
         ts("f2", f, "raw", a, 512, .5, .5, OP.mult, 132 - .25, OP.add)
-        ts("f4", f, "raw", a, 512, .5, .25, OP.mult, 131 - .375, OP.add)
-        ps, terms = newbank(), [("i2", "f2", f), ("i8", "f4", f), ("i32", "f8", f)]
-        if a not in CONV_A:
-            ts("f8", f, "raw", a, 512, .5, 8.0, OP.is_ge, -37.0, OP.add)
+        ts("f8", f, "raw", a, 512, .5, 8.0, OP.is_ge, -37.0, OP.add)
+        ps, terms = newbank(), [("i2", "f2", f), ("i8", "Y", f), ("i32", "f8", f)]
+        if a not in K["CONV_A"]:
             mm(ps, terms, 512)
             tt("win", a, "raw", a, ps, 0, 512, 1, OP.add)
         else:
-            act("f8", f, "raw", a, 512, AF.Copy, .125, 129 - .4375)
-            mm(ps, [("i1", "raw", a)] + terms, 512)
-            act("win", a, ps, 0, 512, AF.Copy, 1.0, 128.0 - 32.0 * (129 + 41))
+            mm(ps, terms + [("i1", "raw", a)], 512)
+            act("win", a, ps, 0, 512)
 
     def ramp(buf, a, n, step, base):
         G(lambda: g.iota(T[buf][:, a:a + n], [[step, n]], base, 0, allow_small_or_imprecise_dtypes=True), n, [("i1", 0, 128)], [(buf, a, a + n)])
 
-    V(lambda: g.vector.memset(T.X[:, S[4] - 2048:S[5] - 2048], 85.0), 256, .5, [], [("X", S[4] - 2048, S[5] - 2048)])
-    for a in range(0, 4096, 512):
+    for a in range(0, 2048, 512):
         ramp("val", a, 512, 1, 4096 + a)
-    ramp("Y", 4096, 16, 0, 256)
-    for a in range(4096, S[5], 1280):
-        ramp("W", a, 1280, 1, 4096 + a)
+    ramp("W", S[2], S[5] - S[2], 1, 2048 + S[2])
     G(lambda: g.affine_select(T.i1f[:], T.onef[:], [[-1, 128]], OP.is_equal, 0.0, 0, 1), 128, [("onef", 0, 128)], [("i1f", 0, 128)])
-    for s in range(16):
-        G(lambda s=s: g.affine_select(T.selm[:, 128 * s:128 * s + 128], T.i1f[:], [[0, 8], [1, 16]], OP.is_equal, 0.0, -s, 0), 128,
-          [("i1f", 0, 128)], [("selm", 128 * s, 128 * s + 128)])
+    op("Y", [lambda k=k: g.sync.dma_start(T.ej[:, 16 * k:16 * k + 16], T.edge[16 * k:16 * k + 16, :]) for k in range(8)], 800, [], [("ej", 0, 128)],
+       lat=16000, dma="ld8", inc=16)
+    ops[-1]["late"] = -9e5
+    ts("ef", 0, "ej", 0, 128, 1)
+    ps = newbank()
+    P([lambda ps=ps: g.tensor.transpose(B[ps][:, 0:128], T.ef[:], T.i1f[:])], 512, [("ef", 0, 128), ("i1f", 0, 128)], [(ps, 0, 512)])
+    ts("ev", 0, ps, 0, 128, 1)
     G(lambda: g.iota(T.kmat[:], [[1, 8], [0, 32]], 0, 0, allow_small_or_imprecise_dtypes=True), 256, [], [("kmat", 0, 256)])
 
-    for a in range(0, 2048, 256):
-        silu("W", 0, 4096, "lo", a // 16, "val", a, 256)
-        silu("W", 0, 4096, "ro", a // 16, "val", 2048 + a, 256)
+    for a in range(0, 2048, K["WCH"]):
+        silu(on("p", a), S[2], (240 if a >= 1024 else 0) + 128 + a % 1024 // 16, "val", a, K["WCH"])
+    for k, w in enumerate(K["WLR"]):
+        for a in range(0, 2048, w):
+            silu(on("q", 2048 * k + a), S[1], 240 * k + a // 16, "W", S[1] + a, w)
 
     for d in range(1, 5):
-        base, nn, n = S[d] - 4096, S[d + 1] - S[d], CHUNK[d]
+        base, nn, n = S[d] - 4096, S[d + 1] - S[d], K["CHUNK"][d]
         for a in range(0, nn, n):
-            c, w, h = base + a, S[d] + a, n // 2
-            bias = -128.0 if d > 2 else 0.0
-            gather(on("l", c), *CA(c), "win", S[d - 1], S[d], "lo", c // 16, n, bias)
-            gather(on("r", c), *CB(c), "win", S[d - 1], S[d], "ro", c // 16, n, bias)
-            double([CA(c), CB(c)], [CA(c + h), CB(c + h)], h, "edge" if d > 2 else "in", "win", w + h, "win", w)
+            c, w = base + a, S[d] + a
+            skew[0] = a * K["SK"][0] if d < 4 else -K["TOP"]
+            gather(on("l", c), *CA(c), "win", 0, S[d], "lr", c // 16, n, -128.0)
+            gather(on("r", c), *CB(c), "win", 0, S[d], "lr", 240 + c // 16, n, -128.0)
+            (single if c in K["UP_1"] else double)([("i1", *CA(c)), ("i1", *CB(c))], n // 2, "win", w, c in K["UP_A"])
 
-    for x, y in (("cb", "lo"), ("ca", "ro")):
-        V(lambda x=x, y=y: g.vector.tensor_copy(T.X[:, S[3] - 2048:S[4] - 2048].indirect(T[y][:, 224:240]), T[x][:, 1536:1792]), 256, SC,
-          [(x, 1536, 1792), (y, 224, 240)], [("X", S[3] - 2048, S[4] - 2048)])
+    skew[0] = 0
+    ts("X", S[4], "win", S[4], 256, .5, 85.0 - 128.0, OP.add)
+    op("G", [lambda: g.dma_start(T.Y[:, 4096:6144], T.Y[:, 2048:4096], accum_op=OP.add)], 1500, [("Y", 2048, 6144)], [("Y", 4096, 6144)], lat=11000, dma="acc", inc=16)
+    for a in range(0, 2048, 512):
+        gather(on("s", a), "s1", a, "Y", 0, 6144, "lr", (240 if a >= 1024 else 0) + 128 + a % 1024 // 16, 512)
+    ps = newbank()
+    mm(ps, [("i1", "ca", 1024), ("i1", "cb", 1024), ("m1", "win", S[3])], 512)
+    out("u3", 0, ps, 512, 128.0)
 
     for q in others + [rank]:
         dst, off = ("land", "cu") if q == rank else ("clout", "cin")
-        gather("A", dst, 512 * q, "win", 0, S[5], off, 32 * q, 512)
-    exchange("clout", "land", 512, "clr", 35000)
+        gather(on("c", q == rank), dst, 512 * q, "win", 0, S[5], off, 32 * q, 512, -128.0)
+    exchange("clout", "land", 512, "clr", K["BACK"])
 
     for a in range(0, 2048, 512):
-        gather("A", "val", a, "W", 0, S[5], "eu", a // 16, 512)
-    ps = newbank()
-    for s in range(16):
-        P([lambda s=s, ps=ps: g.tensor.matmul(T[ps][:, 0:128], T.selm[:, 128 * s:128 * s + 128], T.val[:, s:2048:16], s == 0, s == 15)],
-          512, [("selm", 128 * s, 128 * s + 128), ("val", 0, 2048)], [(ps, 0, 512)])
-    ts("e2", 0, ps, 0, 128, 1, -4095.75, OP.add, 4096.25, OP.min)
-    ts("ek", 0, ps, 0, 128, 1, 6143.5, OP.is_ge, -2048.0, OP.mult)
-    tt("el", 0, "ek", 0, ps, 0, 128, 1, OP.add)
+        gather(on("w", a), "val", a, "W", 0, S[5], "ev", a // 16, 512)
+    ts("ek", 0, "ci", 128, 128, 1, S[1] - .5, OP.is_ge, 2048.0, OP.mult)
+    ts("ek", 128, "ci", 128, 128, 1, S[2] - .5, OP.is_ge, -2048.0, OP.mult)
+    tt("el", 0, "ek", 0, "ek", 128, 128, 2, OP.add)
+    op("G", [lambda: g.dma_start(T.el[:], T.val[0:128:16, :], accum_op=OP.add)], 1000, [("val", 0, 2048), ("el", 0, 128)], [("el", 0, 128)], lat=K["TURN"], dma="ac2", inc=16)
+    skew[0] = -K["TOP"]
     ts("e1", 0, "el", 0, 128, 1, -4095.75, OP.add)
+    skew[0] = 0
 
-    for d in (3, 2, 1):
-        base, nn, n, h = S[d] - 4096, S[d + 1] - S[d], *((1024, 512) if d == 1 else (512, 256))
-        lo_, hi_ = S[d - 1] - 2048, S[d] - 2048
-        for a in range(0, nn, n):
-            c, w = base + a, S[d] + a - 2048
-            if d < 3:
-                (double_a if (d, a) in BY_A else double)([("X", w)], [("X", w + h)], h, "out" if d == 2 else "edge", *OO(c + h), *OO(c))
-            if d > 1:
-                q = c - 2048
-                ob, oa = OO(c)
-                for off, sib in (("lo", "cb"), ("ro", "ca")):
-                    V(lambda off=off, sib=sib, c=c, q=q, n=n, lo_=lo_, hi_=hi_, ob=ob, oa=oa: g.vector.tensor_tensor(
-                        T.X[:, lo_:hi_].indirect(T[off][:, c // 16:(c + n) // 16]), T[ob][:, oa:oa + n], T[sib][:, q:q + n], OP.add), n, SC,
-                      [(ob, oa, oa + n), (sib, q, q + n), (off, c // 16, (c + n) // 16)], [("X", lo_, hi_)])
+    for d, x, x0, y, y0 in ((4, "ca", 1536, "cb", 1536), (3, "X", S[3], "u3", 0)):
+        n = min(K["DOWN"][3], S[d + 1] - S[d])
+        for a in range(0, S[d + 1] - S[d], n):
+            for off, c in (("lr", 0), ("lr", 240)):
+                c += (S[d] - 4096 + a) // 16
+                V(lambda off=off, d=d, c=c, n=n, x=x, xa=x0 + a, y=y, ya=y0 + a: g.vector.tensor_tensor(
+                    T.X[:, 0:S[d]].indirect(T[off][:, c:c + n // 16]), T[x][:, xa:xa + n], T[y][:, ya:ya + n], OP.add), n, SC,
+                  [(x, x0 + a, x0 + a + n), (y, y0 + a, y0 + a + n), (off, c, c + n // 16)], [("X", 0, S[d])])
+        if d == 4:
+            gate[0] = len(ops) - 1
+    n = K["DOWN"][2]
+    for a in range(0, 1024, n):
+        skew[0] = a * K["SK"][1]
+        (single if (2, a) in K["DN_1"] else double)([("m1", "win", S[2] + a), ("i1", "X", S[2] + a)], n // 2, "X", 4096 + a, True, 0.0,
+                                                    [("ca", a), ("cb", a)], 128, K["E2"])
+        if a == K["G1"]:
+            first = len(ops) - 2
+    gate[0] = first
+    n = K["DOWN"][1]
+    for a in range(0, 1024, n):
+        for k, own in enumerate(("ca", "cb")):
+            skew[0] = (2 * a + k * n) * K["SK"][1]
+            (single if (1, a, k) in K["DN_1"] else double)([("m1", own, a), ("i1", "X", 4096 + a)], n // 2, "X", 2048 + 1024 * k + a, True, 0.0,
+                                                           [("s1", 1024 * k + a)], 0, K["E1"])
+    skew[0], gate[0] = 0, len(ops) - 2
+    op("Y", [lambda: g.sync.dma_start(T.X[:, 5120:6144], T.X[:, 4096:5120])], 100, [("X", 4096, 5120)], [("X", 5120, 6144)], lat=2500, dma="dup", inc=16)
 
     def sel(d0, s0, src, pat, o, base, cm):
         G(lambda: g.affine_select(T.gsum[:, d0:d0 + 32], T[src][:, s0:s0 + 32], pat, o, 0.0, base, cm), 32, [reg(src, s0, 32)], [("gsum", d0, d0 + 32)])
 
-    sel(128, 0, "one", [[-16, 8], [0, 4]], OP.is_ge, 0, 1)
-    sel(160, 128, "gsum", [[16, 8], [0, 4]], OP.is_ge, 15, -1)
-    ts("gsum", 128, "gsum", 160, 32, 1, 8.0, OP.mult)
+    fill("eight", 0, 128, 0, 32, 8.0)
+    sel(160, 0, "eight", [[-16, 8], [0, 4]], OP.is_ge, 0, 1)
+    sel(128, 160, "gsum", [[16, 8], [0, 4]], OP.is_ge, 15, -1)
     for b in range(4):
         sel(32 * b, 128, "gsum", [[0, 8], [1, 4]], OP.is_equal, -b, 0)
 
     blocks, n, mid, mid2 = range(0, 2048, 512), 256, {}, {}
     for a in blocks:
-        gather("A", "ine", a, "win", 0, S[5], "eu", a // 16, 512)
-    for a in blocks:
-        gather("A", "ye", a, "Y", 0, 4112, "e2", a // 16, 512, -256.0)
-    for a in blocks:
-        if a in BY_V:
-            V(lambda a=a: g.vector.tensor_tensor(T.ole[:, a:a + 512], T.X[:, 0:S[5] - 2048].indirect(T.e1[:, a // 16:a // 16 + 32]), T.ye[:, a:a + 512], OP.add), 512, GA,
-              [("X", 0, S[5] - 2048), ("e1", a // 16, a // 16 + 32), ("ye", a, a + 512)], [("ole", a, a + 512)])
+        gather(on("i", a), "ine", a, "win", 0, S[5], "cu", 128 + a // 16, 512, -128.0)
+
+    def outer(a, n):
+        w, c = 2 * n, a // 16
+        if a in K["BY_V"]:
+            V(lambda: g.vector.tensor_tensor(T.ole[:, a:a + w], T.X[:, 2048:S[5]].indirect(T.e1[:, c:c + w // 16]), T.ine[:, a:a + w], OP.subtract), w, GA,
+              [("X", 2048, S[5]), ("e1", c, c + w // 16), ("ine", a, a + w)], [("ole", a, a + w)])
         else:
-            gather("A", "ole", a, "X", 0, S[5] - 2048, "e1", a // 16, 512)
-    for a in blocks:
-        sum_ = lambda x: [("ole", x)] + ([] if a in BY_V else [("ye", x)])
-        if a in BY_MAX:
-            o = double(sum_(a), sum_(a + n), n, "edge", "uh", None, "ul", None)
-        else:
-            ph, pl, o = pair(sum_(a), sum_(a + n), n, "edge", "ke", a not in BY_REL, False)
-            if a in BY_REL:
-                act("uh", o, ph, 0, n, AF.Relu, 1.0, 128 * 256.0)
-            else:
-                tt("uh", o, "tY", o, ph, 0, n, 1, OP.max)
-            act("ul", o, pl, 0, n, AF.Relu, 1.0, 128 * 256.0)
-        mid[a] = o
-    for a in blocks:
-        h, o = a + n, mid[a]
-        tl = [] if a in BY_MAX else [("tB", o)]
-        th = [("tY", o)] if a in BY_REL else []
-        ph, pl, o2 = pair([("ine", a), ("ul", o)] + tl, [("ine", h), ("uh", o)] + th, n, "in", "ku", False, False)
-        act("uh", o2, ph, 0, n, AF.Relu, 1.0, 127 * 256.0)
-        act("ul", o2, pl, 0, n, AF.Relu, 1.0, 127 * 256.0)
-        mid2[a] = o2
-    for a in blocks:
-        h, o2 = a + n, mid2[a]
-        o = split([("land", a), ("tB", o2), ("ul", o2)], [("land", h), ("uh", o2), ("tY", o2)], n, "test", a)
-        act("zz", h, "tY", o, n, AF.Relu, -1.0, 129.0)
+            gather("A", "ole", a, "X", 2048, S[5], "e1", c, w)
+        terms = ([] if a in K["BY_V"] else [("m1", "ine", a)]) + [("i1", "ole", a)]
+        double(terms, n, "s2", a, True, 0.0, [("ine", a)], 0, 0 if a in K["BY_V"] else K["E0"])
+
+    def edge(a, n):
+        mid2[a] = split([("i1", "s2", a)], n, "pure")
+
+    def test(a, n):
+        o = split([("i1", "s2", a), ("i1", "land", a)], n, "test", mid2[a], a)
+        act("zz", a + n, "tt", 2 * o + n, n, AF.Relu, -2.0 ** -PB, 1.0)
         ps = newbank()
         fns = []
-        for kk in range(2):
+        for kk in range(n // 128):
             k = a // 256 + kk
             for b in range(4):
-                fns.append(lambda kk=kk, b=b, ps=ps, a=a: g.tensor.matmul(
-                    T[ps][0:32, 64 * kk:64 * kk + 64], T.gsum[:, 32 * b:32 * b + 32],
+                fns.append(lambda kk=kk, b=b: g.tensor.matmul(
+                    B[ps][0:32, 64 * kk:64 * kk + 64], T.gsum[:, 32 * b:32 * b + 32],
                     T.zz[:, a + 256 * kk + 64 * b:a + 256 * kk + 64 * b + 64], b == 0, False))
-            fns.append(lambda kk=kk, k=k, ps=ps: g.tensor.matmul(
-                T[ps][0:32, 64 * kk:64 * kk + 64], T.kmat[:, 32 * k:32 * k + 32], T.inv[:], False, True))
-        P(fns, 64, [("gsum", 0, 128), ("zz", a, a + 512), ("kmat", 0, 256), ("inv", 0, 64)], [(ps, 0, 512)])
-        r = a // 4
-        if a == 0:
-            A(lambda ps=ps: g.scalar.activation(T.key[:, 0:128], T[ps][0:32, 0:128], AF.Copy), 128, 1, [(ps, 0, 512)], [("key", 0, 128)])
-        else:
-            V(lambda ps=ps, r=r: g.vector.tensor_tensor(T.key[:, r:r + 128], T.key[:, r - 128:r], T[ps][0:32, 0:128], OP.min), 128, 1,
-              [(ps, 0, 512), ("key", r - 128, r)], [("key", r, r + 128)])
-    tt("keyi", 0, "key", 384, "key", 448, 64, 2, OP.min)
+            fns.append(lambda kk=kk, k=k: g.tensor.matmul(
+                B[ps][0:32, 64 * kk:64 * kk + 64], T.kmat[:, 32 * k:32 * k + 32], T.inv[:], False, True))
+        P(fns, 64, [("gsum", 0, 128), ("zz", a, a + 2 * n), ("kmat", 0, 256), ("inv", 0, 64)], [(ps, 0, 512)])
+        for kk in range(n // 128):
+            k = a // 256 + kk
+            if k == 0:
+                A(lambda: g.scalar.activation(T.key[:, 0:64], B[ps][0:32, 0:64], AF.Copy), 64, 1, [(ps, 0, 512)], [("key", 0, 64)])
+            else:
+                dst, r = ("key", 64 * k) if k < 7 else ("keyi", 0)
+                V(lambda kk=kk, k=k, dst=dst, r=r: g.vector.tensor_tensor(T[dst][:, r:r + 64], T.key[:, 64 * k - 64:64 * k], B[ps][0:32, 64 * kk:64 * kk + 64], OP.min),
+                  64, 1, [(ps, 0, 512), ("key", 64 * k - 64, 64 * k)], [(dst, r, r + 64)])
+
+    parts = [(sum(K["PARTS"][:k]), w // 2) for k, w in enumerate(K["PARTS"])]
+    for step in range(len(parts) + 2):
+        for k, stage in reversed(list(enumerate((outer, edge, test)))):
+            if 0 <= step - k < len(parts):
+                skew[0] = parts[step - k][0] * K["SK"][2]
+                stage(*parts[step - k])
+    skew[0] = 0
     ts("keyi", 64, "keyi", 0, 64, 1, 3, OP.logical_shift_right)
     ts("keyi", 128, "keyi", 0, 64, 1, 7, OP.bitwise_and)
     ts("res", 0, "keyi", 64, 64, 1)
     ts("res", 64, "keyi", 128, 64, 1)
-    op("Y", [lambda: g.sync.dma_start(T.cost[:], T.res[:, 0:64])], 120, [("res", 0, 64)], [], lat=2000, dma="ld8", inc=16)
-    op("A", [lambda: g.scalar.dma_start(T["first"][:], T.res[:, 64:128])], 120, [("res", 64, 128)], [], lat=2000, dma="ld9", inc=16)
+    op("Y", [lambda: g.sync.dma_start(T.cost[:], T.res[:, 0:64])], 120, [("res", 0, 64)], [], lat=2000, dma="ld10", inc=16)
+    op("A", [lambda: g.scalar.dma_start(T["first"][:], T.res[:, 64:128])], 120, [("res", 64, 128)], [], lat=2000, dma="ld11", inc=16)
 
-    run(g, T, ops)
+    run(g, T, ops, B, hold)
 
 
-def run(g, T, ops):
-    n = len(ops)
+def run(g, T, ops, B, hold):
+    n, hop = len(ops), K["HOP"]
     deps = [dict() for _ in ops]
     hist = {}
     for i, o in enumerate(ops):
+        if "after" in o:
+            deps[i][o["after"]] = ops[o["after"]]["eng"] not in ("G", o["eng"])
         for kind, regs in (("R", o["R"]), ("W", o["W"])):
             for r in regs:
                 psum = r[0][:2] == "ps"
@@ -377,7 +460,7 @@ def run(g, T, ops):
                     same = ops[j]["eng"] == o["eng"]
                     if not w and kind == "R" and (same or not psum):
                         continue
-                    hard = (w and kind == "R") or not same or ops[j]["dma"] is not None or o["eng"] != "P"
+                    hard = (w and kind == "R") or not same or ops[j]["dma"] is not None or (o["eng"] != "P" and K["WAW"])
                     deps[i][j] = deps[i].get(j, False) or hard
         for r in o["R"]:
             hist.setdefault(r[0], []).append((r[1], r[2], i, False))
@@ -388,33 +471,152 @@ def run(g, T, ops):
     for i in range(n):
         for j in deps[i]:
             succ[j].append(i)
-    tail = [0.0] * n
-    for i in range(n - 1, -1, -1):
-        tail[i] = ops[i]["cost"] + ops[i]["lat"] + max([tail[k] + 80 for k in succ[i]] or [0.0])
-    for i in range(n):
-        tail[i] -= ops[i].get("late", 0)
-    free, fin = {}, [0.0] * n
-    need = [len(d) for d in deps]
-    ready = [i for i in range(n) if not need[i]]
-    est = dict((i, 0.0) for i in ready)
-    order = []
-    while ready:
-        best = min(ready, key=lambda i: max(est[i], free.get(ops[i]["eng"], 0.0) if ops[i]["eng"] else 0.0))
-        e = ops[best]["eng"]
-        bt = max(est[best], free.get(e, 0.0) if e else 0.0)
-        if e:
-            cand = [i for i in ready if ops[i]["eng"] == e and max(est[i], free.get(e, 0.0)) <= bt + 60]
-            best = max(cand, key=lambda i: (tail[i], -i))
-            bt = max(est[best], free.get(e, 0.0))
-            free[e] = bt + ops[best]["cost"]
-        fin[best] = bt + ops[best]["cost"] + ops[best]["lat"]
-        order.append(best)
-        ready.remove(best)
-        for k in succ[best]:
-            need[k] -= 1
-            if not need[k]:
-                ready.append(k)
-                est[k] = max(fin[j] + 80 for j in deps[k])
+    cost, lat, eng = [o["cost"] for o in ops], [o["lat"] for o in ops], [o["eng"] for o in ops]
+    users, bank = {}, [None] * n
+    for i, o in enumerate(ops):
+        for r in o["R"] + o["W"]:
+            if r[0][:2] == "ps":
+                bank[i] = r[0]
+        if bank[i]:
+            users.setdefault(bank[i], []).append(i)
+
+    gap = lambda j, k: (K["OWN"] if eng[j] == eng[k] else hop) if deps[k][j] else 0
+
+    def forward(tail):
+        free, fin, order, done = {None: 0.0}, [0.0] * n, [], [False] * n
+        need = [len(d) for d in deps]
+        ready = [i for i in range(n) if not need[i]]
+        est = dict((i, 0.0) for i in ready)
+        left = dict((b, len(u)) for b, u in users.items())
+        spare, place, before = [(0.0, "pb%d" % k, []) for k in range(8)], {}, {}
+        todo = dict((e, [i for i in range(n) if eng[i] == e]) for e in set(eng))
+
+        def start(i):
+            t = max(est[i], free.get(eng[i], 0.0))
+            if bank[i] and bank[i] not in place:
+                if len(spare) <= hold[bank[i]]:
+                    return 1e18
+                t = max(t, min(spare)[0] + hop)
+            return t
+
+        def soon(i, depth):
+            if i in est:
+                return min(start(i), est[i] + 1000)
+            if not depth:
+                return 1e18
+            return max(fin[j] if done[j] else soon(j, depth - 1) + cost[j] + lat[j] for j in deps[i]) + hop
+
+        while ready:
+            best = min(ready, key=start)
+            e, bt = eng[best], start(best)
+            if e:
+                best = max([i for i in ready if eng[i] == e and start(i) <= bt + K["WIN"]], key=lambda i: (tail[i], -i))
+                bt = start(best)
+                if cost[best] > 300:
+                    t = min([soon(i, K["LOOK"]) for i in todo[e] if tail[i] > tail[best] + K["URG"]] or [1e18])
+                    if bt < t < bt + K["FR"] * cost[best]:
+                        free[e] = t
+                        continue
+                free[e] = bt + cost[best]
+            done[best], fin[best], b = True, bt + cost[best] + lat[best], bank[best]
+            todo[e].remove(best)
+            if b:
+                if b not in place:
+                    x = min(spare)
+                    spare.remove(x)
+                    place[b], before[best] = x[1], x[2]
+                left[b] -= 1
+                if not left[b]:
+                    spare.append((max(fin[j] for j in users[b]), place[b], users[b]))
+            order.append(best)
+            ready.remove(best)
+            for k in succ[best]:
+                need[k] -= 1
+                if not need[k]:
+                    ready.append(k)
+                    est[k] = max(fin[j] + gap(j, k) for j in deps[k])
+        return max(fin) + K["ROB"] * sum(replay(order, before, k) for k in range(3)), order, fin, place, before
+
+    def replay(order, before, k):
+        free, fin = {}, [0.0] * n
+        for i in order:
+            t = max([free.get(eng[i], 0.0)] + [fin[j] + gap(j, i) for j in deps[i]] + [fin[j] + hop for j in before.get(i, ())])
+            if k == 2:
+                t += cost[i] * (1 if eng[i] else 2)
+            else:
+                t += cost[i] + ops[i].get("more", (0, 0))[k]
+            if eng[i]:
+                free[eng[i]] = t
+            fin[i] = t + lat[i] * (2 if k == 2 else 1)
+        return max(fin) * (.8, 1.1, .9)[k]
+
+    def backward(fin):
+        free, back = {None: 0.0}, [0.0] * n
+        need = [len(x) for x in succ]
+        ready = [i for i in range(n) if not need[i]]
+        est = dict((i, lat[i]) for i in ready)
+        start = lambda i: max(est[i], free.get(eng[i], 0.0))
+        while ready:
+            best = min(ready, key=start)
+            e, bt = eng[best], start(best)
+            if e:
+                best = max([i for i in ready if eng[i] == e and start(i) <= bt + K["WIN"]], key=lambda i: (fin[i], i))
+                bt = start(best)
+                free[e] = bt + cost[best]
+            back[best] = bt + cost[best]
+            ready.remove(best)
+            for k in deps[best]:
+                need[k] -= 1
+                if not need[k]:
+                    ready.append(k)
+                    est[k] = max(back[j] + gap(k, j) for j in succ[k]) + lat[k]
+        return back
+
+    if "plan" not in PLAN:
+        tail = [0.0] * n
+        for i in range(n - 1, -1, -1):
+            tail[i] = cost[i] + lat[i] + max([tail[k] + hop for k in succ[i]] or [0.0])
+        tail = [tail[i] - ops[i]["late"] for i in range(n)]
+        plans = []
+        for rnd in range(K["ROUNDS"]):
+            plan = forward(tail)
+            plans.append((plan[0], rnd, plan, tail))
+            back = backward(plan[2])
+            tail = [back[i] - (ops[i]["late"] if ops[i]["late"] < K["CUT"] else 0) for i in range(n)]
+        plan, tail = min(plans)[2:]
+        pairs, rnd = [], 0
+        while rnd < K["MORE"]:
+            end, order, fin, place, before = plan
+            prev, last, pairs = {}, {}, []
+            for i in order:
+                prev[i], last[eng[i]] = last.get(eng[i]) if eng[i] else None, i
+            i = max(order, key=lambda x: fin[x])
+            while i is not None:
+                t, j = fin[i] - cost[i] - lat[i], prev[i]
+                near = max(list(deps[i]) + before.get(i, []) + [None], key=lambda x: -1e9 if x is None else fin[x])
+                if j is not None and j not in deps[i] and (near is None or fin[near] + hop < t - 1):
+                    pairs.append((i, j))
+                    i = j
+                else:
+                    i = near
+            for k in range(len(pairs)):
+                i, j = pairs[(7 * rnd + 3) % len(pairs)]
+                rnd += 1
+                new = list(tail)
+                new[i], new[j] = max(tail[i], tail[j]) + K["UP"], min(tail[i], tail[j]) - K["UP"] * (rnd % 3)
+                other = forward(new)
+                if other[0] <= plan[0] + K["TOL"] and other[1] != plan[1]:
+                    plan, tail = other, new
+                    plans.append((plan[0], K["ROUNDS"] + rnd, plan))
+                    break
+        PLAN["plan"] = min(plans)[2]
+        PLAN["all"] = [int(p[0]) for p in plans[:5]] + [len(plans), int(min(plans)[0])]
+    end, order, fin, place, before = PLAN["plan"]
+    for b in place:
+        B[b] = T[place[b]]
+    for i in before:
+        for j in before[i]:
+            deps[i][j] = deps[i].get(j, False) or eng[j] != eng[i]
     queue = {"V": g.vector, "A": g.scalar, "P": g.tensor, "G": g, "Y": g.sync}
     csem = {"V": "qV", "A": "qA", "P": "qP", "G": "qG"}
     total, val = {}, [None] * n

@@ -2,61 +2,32 @@ from concourse.bass import DstId, RemoteDMATransfer
 from concourse.mybir import AluOpType as OP, ActivationFunctionType as AF
 
 S = [0, 4096, 6144, 7168, 7680, 7936]
-NT = 24
+NT = 28
 PB = 16
 K = {
-    "CHUNK": {1: 512, 2: 512, 3: 256, 4: 256},
-    "DOWN": {3: 512, 2: 512, 1: 512},
-    "GA": 1.56, "SC": 3.8, "PE": .45,
-    "LATE": 0,
-    "WCH": 256,
-    "UP_A": (),
-    "BY_A": (0, 512, 1024, 1536),
-    "BY_V": (0, 1024),
-    "EV1": (512, 1536),
-    "EV2": (0, 512, 1024, 1536),
-    "CONT": True,
-    "CONV_A": (512, 1536, 2560, 3584),
-    "F8_A": (),
-    "ON_V": (("r", 0), ("r", 1024), ("r", 2048), ("r", 3072), ("r", 3328), ("r", 3584)),
-    "LOADS": (("Y", "leaf", 0), ("A", "left", 0), ("A", "right", 0), ("Y", "leaf", 1), ("Y", "leaf", 2), ("Y", "leaf", 3), ("A", "clade", 0), ("Y", "edge", 0)),
-    "T0": 2000, "DT": 500, "WIN": 60, "HOP": 80, "KEEP": 3, "LOOK": 2, "URG": 3000, "FR": .6, "SK": (1, 1, 4), "ROUNDS": 5, "CUT": 0, "TOP": 20000,
+    "CONV": (256,) * 8, "CONV_A": (512, 1536),
+    "UP": {1: 512, 2: 256, 3: 256, 4: 256},
+    "UP_A": (), "BY_V": (0, 1536), "WCH": 256, "WLR": (512, 512), "E0": 3, "HELD": 3, "AFTER": 1, "SENDS": ((0, 1, 2),),
+    "ON_V": tuple(("r", a) for a in (0, 512, 1024, 2048, 2304, 2560, 2816, 3072, 3328, 3584)) + (("s", 0), ("s", 512), ("X", 8448), ("X", 9472)),
+    "LOADS": (("Y", "leaf", (0, 1024)), ("A", "left", 0), ("A", "right", 0), ("Y", "leaf", (1024, 1024)),
+              ("Y", "leaf", (2048, 1024)), ("Y", "leaf", (3072, 1024)), ("A", "clade", 0), ("Y", "edge", 0)),
+    "FIX": (30, 140, 70), "GA": 1.4, "SC": 3.2, "PE": .35, "HOP": 180, "OWN": 180, "T0": 1500, "DT": 350, "DMA": 2300,
+    "SK": (1, 2), "EARLY": 30000, "FIRST": 45000, "TOP": 3000, "FP": (8, 6), "RIGHT": (), "ORDER": ((0, 0), (1, 0), (0, 512), (1, 512)), "FEED": 300, "CSK": .5, "CONST": 0, "TURN": 3500, "BACK": 5000,
+    "WIN": 60, "KEEP": 1, "DEEP": 4, "LOOK": 2, "URG": 1000, "FR": .8, "ROUNDS": 5, "MORE": 120, "UP1": 100, "ROB": 1, "TRIES": 0, "HOT": 80,
 }
-K.update(SK=(.5, .5, 3), ON_V=(("r", 0), ("r", 2048), ("r", 2304), ("r", 2560), ("r", 3072), ("r", 3328), ("r", 3584)),
-         CHUNK={1: 512, 2: 256, 3: 256, 4: 256}, LATE=15000, FR=.8, DOWN={3: 256, 2: 256, 1: 512}, KEEP=2, TOP=3000, UP_A=(0, 3584), BY_A=(0, 512, 1024), BY_V=(0, 1536),
-         CONV_A=(0, 512, 1536, 2560, 3072))
-K.update(HOP=150, PE=.38, T0=1600, DT=400, GA=1.45, SC=3.6, WAW=True, EARLY=3000, UP_1=(), DN_1=(), URG=1500, DOWN={3: 512, 2: 256, 1: 512})
-K.update(WAW=True, UP_A=(0, 512, 1024, 2048, 3584), DN_1=((2, 0), (1, 1536)), BY_V=(0, 1024), HOP=160,
-         ON_V=(("r", 0), ("r", 1024), ("r", 2048), ("r", 2304), ("r", 2560), ("r", 3072), ("r", 3328), ("r", 3584)))
-K.update(WLR=(256, 256), E1=0, E2=0, DN_1=(), DOWN={3: 512, 2: 256, 1: 512})
-K.update(UP_A=(3584,), LATE=0, EARLY=30000, WLR=(256, 512),
-         ON_V=tuple(("r", a) for a in (0, 512, 1024, 2048, 2304, 2560, 2816, 3072, 3328, 3584)) + tuple(("s", a) for a in (0, 512, 1024, 1536)) + (("w", 0), ("w", 512)))
-K.update(DEEP=4, G1=0, E0=3, E2=3, MORE=300, TOL=0, UP=100, PARTS=(512, 512, 512, 256, 256))
-K.update(ROB=.5, OWN=110, CONV_P=(), PARTS=(512,) * 4, PE=.31, SC=3.2, GA=1.4, MORE=0, HOP=150, DOWN={3: 512, 2: 512, 1: 512}, CONV_A=(0, 512, 1024, 1536, 2048, 2560),
-         ON_V=tuple(("r", a) for a in (0, 1024, 2048, 2304, 2560, 3072, 3328, 3584)) + tuple(("s", a) for a in (0, 512, 1024, 1536)) + (("w", 0), ("w", 512)))
-K.update(MORE=300, ON_V=K["ON_V"] + (("r", 512), ("r", 2816)))
-K.update(FIX=(48, 68), FIRST=45000, BACK=6000)
-K.update(E0=0, E2=0, MORE=0, ROB=0, HOP=160, OWN=160, PE=.38, GA=1.45, SC=3.6, FIX=(35, 50, 50), DOWN={3: 512, 2: 256, 1: 512}, CONV_A=(0, 512, 1536, 2560, 3072))
-K.update(FIX=(30, 195, 72), PE=.355, GA=1.56, SC=3.8, HOP=90, OWN=70, ROB=.5, DOWN={3: 512, 2: 512, 1: 512}, E2=3, UP_A=())
-K.update(MORE=100, CONV_A=(0, 1536, 2560), ON_V=tuple(("r", a) for a in (0, 1024, 2048, 2304, 2560, 3072, 3328, 3584))
-         + (("X", 4096), ("X", 4608), ("X", 2560), ("X", 3584), ("u3", 0)) + tuple(("s", a) for a in (0, 512, 1024, 1536)))
-K.update(MORE=0, HOP=200, OWN=180, FIX=(25, 160, 70), PE=.33, GA=1.4, SC=3.2)
-K.update(E2=0, E0=3, CONV_A=(0, 512, 1536, 2560, 3072), ON_V=tuple(("r", a) for a in (0, 512, 1024, 2048, 2304, 2560, 2816, 3072, 3328, 3584))
-         + tuple(("s", a) for a in (0, 512, 1024, 1536)) + (("w", 0), ("w", 512)))
-K.update(TURN=3500, BY_V=(0,), MORE=100, ON_V=K["ON_V"] + tuple(("X", 2048 + a) for a in (0, 1024, 512, 1536)))
-K.update(WLR=(512, 512), MORE=250, ROB=1, E2=3)
+K.update(CONV_A=(512,), RIGHT=(512,), GA=1.55, SC=3.8, FEED=0, FR=.9, MORE=100, ROB=2, ON_V=K["ON_V"] + (("s", 1536), ("r", 1536)))
 PLAN = {}
 
 BUFS = {
-    "bfloat16": {"raw": 4096, "f2": 2048, "f8": 2048, "win": 7936, "X": 7936, "eight": 32, "Y": 6144, "ca": 1792, "cb": 1792,
-                 "u3": 512, "tt": 512 * NT, "s1": 2048, "s2": 2048,
-                 "ole": 2048, "ine": 2048, "zz": 2048, "land": 2048, "clout": 2048, "one": 512, "gsum": 192,
-                 "ke": 128, "kmat": 256, "inv": 64},
-    "float32": {"key": 512, "res": 128, "W": 7936, "val": 2048, "ek": 256, "el": 128, "onef": 128, "i1f": 128, "ef": 128},
+    "bfloat16": {"raw": 2048, "win": 7936, "X": 12032, "Y": 6144, "ca": 1792, "cb": 1792, "u3": 512, "sb": 2048, "tt": 512 * NT, "s1": 2048, "s2": 2048,
+                 "ole": 2048, "ine": 2048, "zz": 2048, "land": 2048, "clout": 2048, "one": 512, "gsum": 192, "eight": 32,
+                 "kc": 128, "ke": 128, "kmat": 256, "inv": 64},
+    "float32": {"key": 512, "res": 128, "W": 7936, "val": 2048, "ek": 256, "el": 128, "i1f": 128, "ef": 128},
     "int32": {"ej": 128, "tS": 256 * NT, "tT": 256 * NT, "li": 480, "ci": 256, "keyi": 192},
     "uint16": {"lr": 480, "cu": 256, "cin": 128, "e1": 128, "ev": 128},
 }
-DIAG = {"i1": 1.0, "m1": -1.0, "mq": -2.0 ** PB, "i2": 2.0, "i8": 8.0, "i32": 32.0, "ik": -256.0, "iq": 2.0 ** PB, "ip": 2.0 ** -PB, "i14": 2.0 ** 14, "kn": -2.0 ** 33, "kp": 2.0 ** 33}
+DIAG = {"i1": 1.0, "m1": -1.0, "iq": 2.0 ** PB, "mq": -2.0 ** PB, "ip": 2.0 ** -PB, "i14": 2.0 ** 14, "ik": -256.0, "kn": -2.0 ** 33, "kp": 2.0 ** 33,
+        "i33": 33.0, "h33": 33.0 * 2 ** 14, "i16": 16.0, "f2": -31.0, "f4": 62.0, "f8": -124.0}
 SCRATCH = {}
 for _t in BUFS:
     for _b in BUFS[_t]:
@@ -65,20 +36,19 @@ for _b in DIAG:
     SCRATCH[_b] = ("sbuf", [128, 128], "bfloat16")
 for _b in range(8):
     SCRATCH["pb%d" % _b] = ("psum", [128, 512], "float32")
-SEMAPHORES = (["qV", "qA", "qP", "qG", "snd", "acc", "ac2", "dup"] + ["ld%d" % i for i in range(12)] + ["lst%d" % i for i in range(4)]
-              + ["clr%d" % i for i in range(4)])
+SEMAPHORES = (["qV", "qA", "qP", "qG", "snd"] + ["d%d" % i for i in range(32)] + ["lst%d" % i for i in range(4)] + ["clr%d" % i for i in range(4)])
 
 
 def rank_program(g, core, T, topo):
     rank = T.rank_of(core)
     if rank is None:
         return
-    others = [q for q in range(len(T.cores)) if q != rank]
-    gate = [None]
-    ops, hold, skew = [], {}, [0]
+    others = [(rank + k) % len(T.cores) for k in range(1, len(T.cores))]
+    ops, hold, skew, gate = [], {}, [0], [None]
     B = dict((b, T[b]) for b in SCRATCH)
     GA, SC = K["GA"], K["SC"]
     RANGE = ({GA: 1.95, SC: 5.3}, {GA: 1.1, SC: 1.9})
+    bank, slots, sems = [0], [0], [0]
 
     def op(eng, fns, cost, R=(), W=(), lat=0.0, dma=None, inc=0, seen=None):
         ops.append({"eng": eng, "fns": fns, "cost": cost, "R": list(R), "W": list(W), "lat": lat, "dma": dma, "inc": inc, "seen": seen,
@@ -93,15 +63,20 @@ def rank_program(g, core, T, topo):
         ops[-1]["more"] = [.83 * n * (x.get(c, c) - c) for x in RANGE]
 
     def P(fns, n, R, W):
-        op("P", fns, 8 + (6 + K["PE"] * max(64, n)) * len(fns), R, W)
+        op("P", fns, K["FP"][0] + (K["FP"][1] + K["PE"] * max(64, n)) * len(fns), R, W)
 
     def G(fn, n, R, W):
         op("G", [fn], 150 + 1.66 * n, R, W)
 
-    on = lambda k, a: "V" if (k, a) in K["ON_V"] else "A"
-    bank, slots = [0], [0]
+    def dma(eng, pairs, R, W, lat=None, add=False):
+        q = {"Y": g.sync, "A": g.scalar, "G": g}[eng]
+        fns = [lambda o=o, i=i: g.dma_start(o, i, accum_op=OP.add) if add else q.dma_start(o, i) for o, i in pairs]
+        op(eng, fns, (1100 if eng == "G" else 100) * len(pairs), R, W, lat=lat or K["DMA"], dma="d%d" % sems[0], inc=16)
+        sems[0] += 1
 
-    def newbank(held=False):
+    on = lambda k, a: "V" if (k, a) in K["ON_V"] else "A"
+
+    def newbank(held=0):
         bank[0] += 1
         hold["ps%d" % bank[0]] = (0, K["KEEP"], K["DEEP"])[held]
         return "ps%d" % bank[0]
@@ -121,8 +96,8 @@ def rank_program(g, core, T, topo):
             fns.append(lambda m=m, b=b, a=a, st=st, sp=sp: g.tensor.matmul(B[ps][:, 0:n], T[m][:, 0:128], T[b][:, a:a + n], st, sp))
         P(fns, n, [(m, 0, 128) for m, b, a in terms] + [(b, a, a + n) for m, b, a in terms], [(ps, 0, 512)])
 
-    def ts(dst, d0, src, s0, n, c, s1=None, op0=None, s2=None, op1=None):
-        o, i = (lambda: B[dst][:, d0:d0 + n]), (lambda: B[src][:, s0:s0 + n])
+    def ts(dst, d0, src, s0, n, c, s1=None, op0=None, s2=None, op1=None, p=128):
+        o, i = (lambda: B[dst][0:p, d0:d0 + n]), (lambda: B[src][0:p, s0:s0 + n])
         if op0 is None:
             fn = lambda: g.vector.tensor_copy(o(), i())
         elif op1 is None:
@@ -135,22 +110,28 @@ def rank_program(g, core, T, topo):
         V(lambda: g.vector.tensor_tensor(B[dst][:, d0:d0 + n], B[x][:, x0:x0 + n], B[y][:, y0:y0 + n], o), n, c,
           [reg(x, x0, n), reg(y, y0, n)], [reg(dst, d0, n)])
 
-    def act(dst, d0, src, s0, n, func=AF.Copy, scale=1.0, bias=0.0):
-        A(lambda: g.scalar.activation(B[dst][:, d0:d0 + n], B[src][:, s0:s0 + n], func, bias=bias, scale=scale), n, 1,
+    def act(dst, d0, src, s0, n, func=AF.Copy, scale=1.0, bias=0.0, p=128):
+        A(lambda: g.scalar.activation(B[dst][0:p, d0:d0 + n], B[src][0:p, s0:s0 + n], func, bias=bias, scale=scale), n, 1,
           [reg(src, s0, n)], [reg(dst, d0, n)])
 
-    def out(dst, d0, ps, n, bias=0.0):
+    def out(dst, d0, src, n, bias=0.0, s0=0):
         if on(dst, d0) == "V":
-            ts(dst, d0, ps, 0, n, 1, *((bias, OP.add) if bias else ()))
+            ts(dst, d0, src, s0, n, 1, *((bias, OP.add) if bias else ()))
         else:
-            act(dst, d0, ps, 0, n, AF.Copy, 1.0, bias)
+            act(dst, d0, src, s0, n, AF.Copy, 1.0, bias)
 
     def fill(buf, p0, p1, a, b, x):
         V(lambda: g.vector.memset(T[buf][p0:p1, a:b], x), b - a, .5, [], [(buf, a, b)])
 
+    def turn(src, c0, rows, cols):
+        ps = newbank()
+        P([lambda: g.tensor.transpose(B[ps][0:cols, 0:rows], T[src][0:rows, c0:c0 + cols], T.i1f[0:rows, 0:rows])], 512,
+          [(src, c0, c0 + cols), ("i1f", 0, 128)], [(ps, 0, 512)])
+        return ps
+
     HIGH = {"i1": "iq", "m1": "mq"}
 
-    def split(terms, n, kind, add=None, z=None, short=0, early=0):
+    def split(terms, n, kind, add=None, z=None, early=0, short=0):
         pp, o, pb = newbank(2 * (early & 1) if add is None else 1), newslot(max(n, 256)), 14 if kind == "edge" else PB
         both = [x for m, b, a in terms for x in (("i14" if kind == "edge" else HIGH[m], b, a + n), (m, b, a))]
         if add is not None:
@@ -160,6 +141,7 @@ def rank_program(g, core, T, topo):
             mm(pp, both[:2], n, stop=False)
             ops[-1]["after"] = gate[0]
         mm(pp, both[2 * (early & 1):], n, start=not early & 1 and add is None)
+        ops[-1]["late"] = min(skew[0], 0) - K["FEED"]
         short += 256 if kind == "edge" else 0
         if add is not None:
             tt("tS", o, "tT", add, pp, 0, n, 1, OP.add)
@@ -172,49 +154,38 @@ def rank_program(g, core, T, topo):
         else:
             ts("tt", 2 * o + n, "tT", o, n, 1, 1.5 * 2.0 ** (23 + pb), OP.add, 1.5 * 2.0 ** (23 + pb), OP.subtract)
         mm(pp, [("i14" if kind == "edge" else "i1", "tt", 2 * o + n)], n)
+        ops[-1]["late"] = min(skew[0], 0) - K["FEED"]
         if kind == "test":
             tt("zz", z, "tT", o, pp, 0, n, 1, OP.is_equal)
         else:
             tt("tt", 2 * o, "tT", o, pp, 0, n, 1, OP.subtract)
         return o
 
-    def absorb(ps, o, n, more=(), stop=True):
+    def absorb(ps, o, n, more=()):
         mm(ps, [("kn", "tt", 2 * o), ("kp", "tt", 2 * o)] + [("i1", b, a) for b, a in more], 2 * n, start=False, stop=False)
         P([lambda: g.tensor.matmul(B[ps][:, 0:n], T.i1[:], T.tt[:, 2 * o:2 * o + n], False, False),
-           lambda: g.tensor.matmul(B[ps][:, n:2 * n], T.ip[:], T.tt[:, 2 * o + n:2 * o + 2 * n], False, stop)], n,
+           lambda: g.tensor.matmul(B[ps][:, n:2 * n], T.ip[:], T.tt[:, 2 * o + n:2 * o + 2 * n], False, True)], n,
           [("i1", 0, 128), ("ip", 0, 128), ("tt", 2 * o, 2 * o + 2 * n)], [(ps, 0, 512)])
 
-    def double(terms, n, dst, d0, by_a, bias=128.0, more=(), short=0, early=0):
-        o, ps = split(terms, n, "pure" if by_a else "edge", short=short, early=early), newbank(2 if early & 2 else 1)
-        terms = ([("one", "one", 0)] if short else []) + ([] if by_a else [("ke", "one", 0)]) + terms
+    def double(terms, n, dst, d0, plain, bias=128.0, more=(), early=0, short=0):
+        o, ps = split(terms, n, "pure" if plain else "edge", early=early, short=short), newbank(2 if early & 2 else 1)
+        terms = ([("one", "one", 0)] if short else []) + ([] if plain else [("ke", "one", 0)]) + terms
         if early & 2:
             mm(ps, terms[:-1], 2 * n, stop=False)
             ops[-1]["after"] = gate[0]
         mm(ps, terms[-1:] if early & 2 else terms, 2 * n, start=not early & 2, stop=False)
-        if by_a:
-            if more and on(dst, d0) == "V":
-                absorb(ps, o, n, more[1:])
-                tt(dst, d0, *more[0], ps, 0, 2 * n, 1, OP.add)
-            else:
-                absorb(ps, o, n, more)
-                out(dst, d0, ps, 2 * n, bias)
-        else:
+        if not plain:
             mm(ps, [("ik", "tt", 2 * o)], 2 * n, start=False)
             tt(dst, d0, "tt", 2 * o, ps, 0, 2 * n, 1, OP.max)
-
-    def single(terms, n, dst, d0, by_a, bias=128.0, more=(), short=0, early=0):
-        pp, o, ps, n = newbank(), newslot(max(2 * n, 256)), newbank(True), 2 * n
-        mm(pp, terms, n)
-        ts("tS", o, pp, 0, n, 1, *((float(short), OP.add) if short else ()))
-        ts("tT", o, "tS", o, n, 1, 1, OP.logical_shift_right, 0x55, OP.bitwise_and)
-        ts("tt", 2 * o, "tT", o, n, 1, *(() if by_a else (128.0, OP.add)))
-        mm(ps, terms + ([("one", "one", 0)] if short else []) + ([] if by_a else [("ke", "one", 0)]), n, stop=False)
-        if by_a:
-            mm(ps, [(m, "tt", 2 * o) for m in ("kn", "kp", "i1")] + [("i1", b, a) for b, a in more], n, start=False)
-            act(dst, d0, ps, 0, n, AF.Copy, 1.0, bias)
+        elif dst is None:
+            absorb(ps, o, n)
+        elif more and on(dst, d0) == "V":
+            absorb(ps, o, n, more[1:])
+            tt(dst, d0, *more[0], ps, 0, 2 * n, 1, OP.add)
         else:
-            mm(ps, [("ik", "tt", 2 * o)], n, start=False)
-            tt(dst, d0, "tt", 2 * o, ps, 0, n, 1, OP.max)
+            absorb(ps, o, n, more)
+            out(dst, d0, ps, 2 * n, bias)
+        return ps
 
     def gather(eng, dst, d0, src, a, b, off, c0, n, bias=0.0):
         ind = lambda: T[src][:, a:b].indirect(T[off][:, c0:c0 + n // 16])
@@ -226,34 +197,46 @@ def rank_program(g, core, T, topo):
         else:
             A(lambda: g.scalar.activation(T[dst][:, d0:d0 + n], ind(), AF.Copy, bias=bias), n, GA, R, W)
 
-    def silu(eng, b, c0, src, s0, n):
+    def scatter(b, c0, src, s0, n):
         to, R = (lambda: T.W[:, 0:b].indirect(T.lr[:, c0:c0 + n // 16])), [(src, s0, s0 + n), ("lr", c0, c0 + n // 16)]
-        if eng == "V":
+        if on("q", c0) == "V":
             V(lambda: g.vector.tensor_copy(to(), T[src][:, s0:s0 + n]), n, SC, R, [("W", 0, b)])
         else:
             A(lambda: g.scalar.activation(to(), T[src][:, s0:s0 + n], AF.Silu), n, SC, R, [("W", 0, b)])
-        ops[-1]["late"] = K["LATE"]
-
-    CA = lambda c: ("Y", 2048 + c) if c < 2048 else ("ca", c - 2048)
-    CB = lambda c: ("Y", 4096 + c) if c < 2048 else ("cb", c - 2048)
 
     SRC = {"leaf": ("raw", 1024, 0), "left": ("li", 240, 0), "right": ("li", 240, 240), "clade": ("ci", 128, 0), "edge": ("ci", 128, 128)}
-    for i, (eng, src, k) in enumerate(K["LOADS"]):
+    for i, (eng, src, a) in enumerate(K["LOADS"]):
         dst, w, d0 = SRC[src]
-        q, d0 = g.sync if eng == "Y" else g.scalar, d0 + k * w
-        op(eng, [lambda q=q, dst=dst, src=src, a=k * w, w=w, d0=d0: q.dma_start(T[dst][:, d0:d0 + w], T[src][:, a:a + w])], 100, [], [(dst, d0, d0 + w)],
-           lat=K["T0"] + K["DT"] * i + {"clade": 1500, "edge": 6000}.get(src, 0), dma="ld%d" % i, inc=16)
-        ops[-1]["late"] = -1e6 + 1e4 * i
+        if src == "leaf":
+            a, w = a
+            dst, d0 = ("Y", a) if a < 2048 else ("raw", a - 2048)
+        skew[0] = -1e6 + 1e4 * i
+        dma(eng, [(T[dst][:, d0:d0 + w], T[src][:, a:a + w])], [], [(dst, d0, d0 + w)], K["T0"] + K["DT"] * i + {"clade": 1500, "edge": 6000}.get(src, 0))
+    skew[0] = -9e5
+    dma("Y", [(T.ej[:, 16 * q:16 * q + 16], T.edge[16 * q:16 * q + 16, :]) for q in range(8)], [], [("ej", 0, 128)], 16000)
+    skew[0] = -K["CONST"]
 
     fill("one", 0, 128, 0, 512, 1.0)
     G(lambda: g.affine_select(T.i1[:], T.one[:, 0:128], [[-1, 128]], OP.is_equal, 0.0, 0, 1), 128, [("one", 0, 128)], [("i1", 0, 128)])
     for nm in DIAG:
         if nm != "i1":
             ts(nm, 0, "i1", 0, 128, .5, DIAG[nm], OP.mult)
+    ts("i1f", 0, "i1", 0, 128, 1)
     fill("ke", 0, 64, 0, 128, 512.0)
     fill("ke", 64, 128, 0, 128, 2.0)
-    fill("onef", 0, 128, 0, 128, 1.0)
+    fill("kc", 0, 64, 0, 128, -2.0 ** 15)
+    fill("kc", 64, 128, 0, 128, -2.0)
     fill("inv", 0, 128, 0, 64, 2.0 ** -7)
+    fill("eight", 0, 128, 0, 32, 8.0)
+    skew[0] = 0
+
+    def ramp(buf, a, n, step, base):
+        G(lambda: g.iota(T[buf][:, a:a + n], [[step, n]], base, 0, allow_small_or_imprecise_dtypes=True), n, [("i1", 0, 128)], [(buf, a, a + n)])
+
+    for a in range(0, 2048, 512):
+        ramp("val", a, 512, 1, 4096 + a)
+    ramp("W", S[2], S[5] - S[2], 1, 4096 - 1792)
+    G(lambda: g.iota(T.kmat[:], [[1, 8], [0, 32]], 0, 0, allow_small_or_imprecise_dtypes=True), 256, [], [("kmat", 0, 256)])
 
     ts("cu", 128, "ci", 128, 128, 1)
     skew[0] = -K["EARLY"]
@@ -261,155 +244,154 @@ def rank_program(g, core, T, topo):
     skew[0] = -K["FIRST"]
     ts("cu", 0, "ci", 0, 128, 1)
 
-    def fused(src, dst, w, sem):
+    def fused(src, dst, w, sem, whom):
         tr = []
-        for i, q in enumerate(others):
-            to = T.cores[q]
+        for q in whom:
+            i, to = others.index(q), T.cores[q]
             rid, pid, _e = topo.addr(to)
             en = topo.engines(core, to)[4 * i:4 * i + 4]
             tr.append(RemoteDMATransfer(dst_ids=[DstId(rid=rid, pnc=pid)], dma_engine_mask=sum(1 << e for e in en),
                                         remote_sem=T.sem[sem + str(rank)], src=T[src][:, w * q:w * q + w],
                                         dst=T[dst][:, w * rank:w * rank + w]))
         g.remote_dma_fused(tr, local_sem=T.sem.snd)
-        return None
 
-    def exchange(src, dst, w, sem, t):
-        op("G", [lambda: fused(src, dst, w, sem)], 1500, [(src, w * q, w * q + w) for q in others], [], lat=2000, dma="snd", inc=12)
+    def exchange(src, dst, w, sem, t, whom, whence):
+        op("G", [lambda: fused(src, dst, w, sem, whom)], 1500, [(src, w * q, w * q + w) for q in whom], [], lat=2000, dma="snd", inc=4 * len(whom))
         me = len(ops) - 1
-        for q in others:
+        for q in whence:
             op(None, [], t, [], [(dst, w * q, w * q + w)], seen=(sem + str(q), 4))
             ops[-1]["after"] = me
 
-    exchange("cu", "cin", 32, "lst", 9000)
+    exchange("cu", "cin", 32, "lst", 9000, others, others)
+
     skew[0] = 0
 
-    for a in range(0, 4096, 512):
-        f = a % 2048
-        ts("Y", f, "raw", a, 512, .5, .25, OP.mult, 131 - .375, OP.add)
-        ts("f2", f, "raw", a, 512, .5, .5, OP.mult, 132 - .25, OP.add)
-        ts("f8", f, "raw", a, 512, .5, 8.0, OP.is_ge, -37.0, OP.add)
-        ps, terms = newbank(), [("i2", "f2", f), ("i8", "Y", f), ("i32", "f8", f)]
-        if a not in K["CONV_A"]:
-            mm(ps, terms, 512)
-            tt("win", a, "raw", a, ps, 0, 512, 1, OP.add)
-        else:
-            mm(ps, terms + [("i1", "raw", a)], 512)
-            act("win", a, ps, 0, 512)
+    for k, n in enumerate(K["CONV"]):
+        a, pp = 2 * sum(K["CONV"][:k]), newbank()
+        raw, r = ("Y", a) if a < 2048 else ("raw", a - 2048)
+        skew[0] = (a // 1024 * 1024 - 4096) * K["CSK"]
+        if a in K["CONV_A"]:
+            f = ("sb", "s2", "ole", "zz")[k % 4]
+            ts(f, 0, raw, r, 512, .5, .5, OP.mult, 132 - .25, OP.add)
+            ts(f, 512, raw, r, 512, .5, .25, OP.mult, 131 - .375, OP.add)
+            ts(f, 1024, raw, r, 512, .5, 8.0, OP.is_ge, -37.0, OP.add)
+            mm(pp, [("f2", f, 0), ("f4", f, 512), ("f8", f, 1024), ("i16", raw, r)], 512)
+            act("win", a, pp, 0, 512, AF.Copy, 1.0, 128.0 + 31 * 132 - 62 * 131 - 124 * 37)
+            continue
+        o = newslot(n)
+        mm(pp, [("h33", raw, r + n), ("i33", raw, r)], n)
+        ts("tS", o, pp, 0, n, 1)
+        ts("tT", o, "tS", o, n, 1, 1, OP.logical_shift_right, 0x55 + (0x55 << 14), OP.bitwise_and)
+        ts("win", a + n, "tT", o, n, 1, 2.0 ** -14, OP.mult, 128.0, OP.add)
+        mm(pp, [("kc", "one", 0), ("i14", "win", a + n)], n)
+        tt("win", a, "tT", o, pp, 0, n, 1, OP.subtract)
 
-    def ramp(buf, a, n, step, base):
-        G(lambda: g.iota(T[buf][:, a:a + n], [[step, n]], base, 0, allow_small_or_imprecise_dtypes=True), n, [("i1", 0, 128)], [(buf, a, a + n)])
-
-    for a in range(0, 2048, 512):
-        ramp("val", a, 512, 1, 4096 + a)
-    ramp("W", S[2], S[5] - S[2], 1, 2048 + S[2])
-    G(lambda: g.affine_select(T.i1f[:], T.onef[:], [[-1, 128]], OP.is_equal, 0.0, 0, 1), 128, [("onef", 0, 128)], [("i1f", 0, 128)])
-    op("Y", [lambda k=k: g.sync.dma_start(T.ej[:, 16 * k:16 * k + 16], T.edge[16 * k:16 * k + 16, :]) for k in range(8)], 800, [], [("ej", 0, 128)],
-       lat=16000, dma="ld8", inc=16)
-    ops[-1]["late"] = -9e5
-    ts("ef", 0, "ej", 0, 128, 1)
-    ps = newbank()
-    P([lambda ps=ps: g.tensor.transpose(B[ps][:, 0:128], T.ef[:], T.i1f[:])], 512, [("ef", 0, 128), ("i1f", 0, 128)], [(ps, 0, 512)])
-    ts("ev", 0, ps, 0, 128, 1)
-    G(lambda: g.iota(T.kmat[:], [[1, 8], [0, 32]], 0, 0, allow_small_or_imprecise_dtypes=True), 256, [], [("kmat", 0, 256)])
-
+    skew[0] = 0
+    place = lambda a: 240 * (a // 1024) + 128 + a % 1024 // 16
     for a in range(0, 2048, K["WCH"]):
-        silu(on("p", a), S[2], (240 if a >= 1024 else 0) + 128 + a % 1024 // 16, "val", a, K["WCH"])
+        scatter(S[2], place(a), "val", a, K["WCH"])
     for k, w in enumerate(K["WLR"]):
         for a in range(0, 2048, w):
-            silu(on("q", 2048 * k + a), S[1], 240 * k + a // 16, "W", S[1] + a, w)
+            scatter(S[1], 240 * k + a // 16, "W", S[1] + a, w)
+    ts("ef", 0, "ej", 0, 128, 1)
+    ts("ev", 0, turn("ef", 0, 128, 128), 0, 128, 1)
 
+    CA = lambda c: ("Y", 2048 + c) if c < 2048 else ("ca", c - 2048)
+    CB = lambda c: ("Y", 4096 + c) if c < 2048 else ("cb", c - 2048)
     for d in range(1, 5):
-        base, nn, n = S[d] - 4096, S[d + 1] - S[d], K["CHUNK"][d]
-        for a in range(0, nn, n):
-            c, w = base + a, S[d] + a
+        n = K["UP"][d]
+        for a in range(0, S[d + 1] - S[d], n):
+            c = S[d] - 4096 + a
             skew[0] = a * K["SK"][0] if d < 4 else -K["TOP"]
             gather(on("l", c), *CA(c), "win", 0, S[d], "lr", c // 16, n, -128.0)
             gather(on("r", c), *CB(c), "win", 0, S[d], "lr", 240 + c // 16, n, -128.0)
-            (single if c in K["UP_1"] else double)([("i1", *CA(c)), ("i1", *CB(c))], n // 2, "win", w, c in K["UP_A"])
-
+            double([("i1", *CA(c)), ("i1", *CB(c))], n // 2, "win", S[d] + a, c in K["UP_A"])
     skew[0] = 0
     ts("X", S[4], "win", S[4], 256, .5, 85.0 - 128.0, OP.add)
-    op("G", [lambda: g.dma_start(T.Y[:, 4096:6144], T.Y[:, 2048:4096], accum_op=OP.add)], 1500, [("Y", 2048, 6144)], [("Y", 4096, 6144)], lat=11000, dma="acc", inc=16)
+    dma("G", [(T.Y[:, 4096:6144], T.Y[:, 2048:4096])], [("Y", 2048, 6144)], [("Y", 4096, 6144)], 11000, True)
     for a in range(0, 2048, 512):
-        gather(on("s", a), "s1", a, "Y", 0, 6144, "lr", (240 if a >= 1024 else 0) + 128 + a % 1024 // 16, 512)
+        gather(on("s", a), "s1", a, "Y", 0, 6144, "lr", place(a), 512)
     ps = newbank()
     mm(ps, [("i1", "ca", 1024), ("i1", "cb", 1024), ("m1", "win", S[3])], 512)
     out("u3", 0, ps, 512, 128.0)
 
-    for q in others + [rank]:
-        dst, off = ("land", "cu") if q == rank else ("clout", "cin")
-        gather(on("c", q == rank), dst, 512 * q, "win", 0, S[5], off, 32 * q, 512, -128.0)
-    exchange("clout", "land", 512, "clr", K["BACK"])
-
     for a in range(0, 2048, 512):
         gather(on("w", a), "val", a, "W", 0, S[5], "ev", a // 16, 512)
-    ts("ek", 0, "ci", 128, 128, 1, S[1] - .5, OP.is_ge, 2048.0, OP.mult)
-    ts("ek", 128, "ci", 128, 128, 1, S[2] - .5, OP.is_ge, -2048.0, OP.mult)
+    for k, x in enumerate((2048.0, -2048.0)):
+        ts("ek", 128 * k, "ci", 128, 128, 1, S[k + 1] - .5, OP.is_ge, x, OP.mult)
     tt("el", 0, "ek", 0, "ek", 128, 128, 2, OP.add)
-    op("G", [lambda: g.dma_start(T.el[:], T.val[0:128:16, :], accum_op=OP.add)], 1000, [("val", 0, 2048), ("el", 0, 128)], [("el", 0, 128)], lat=K["TURN"], dma="ac2", inc=16)
+    dma("G", [(T.el[:], T.val[0:128:16, :])], [("val", 0, 2048), ("el", 0, 128)], [("el", 0, 128)], K["TURN"], True)
     skew[0] = -K["TOP"]
-    ts("e1", 0, "el", 0, 128, 1, -4095.75, OP.add)
+    ts("e1", 0, "el", 0, 128, 1, 1792 - 4095.75, OP.add)
     skew[0] = 0
 
-    for d, x, x0, y, y0 in ((4, "ca", 1536, "cb", 1536), (3, "X", S[3], "u3", 0)):
-        n = min(K["DOWN"][3], S[d + 1] - S[d])
-        for a in range(0, S[d + 1] - S[d], n):
-            for off, c in (("lr", 0), ("lr", 240)):
-                c += (S[d] - 4096 + a) // 16
-                V(lambda off=off, d=d, c=c, n=n, x=x, xa=x0 + a, y=y, ya=y0 + a: g.vector.tensor_tensor(
-                    T.X[:, 0:S[d]].indirect(T[off][:, c:c + n // 16]), T[x][:, xa:xa + n], T[y][:, ya:ya + n], OP.add), n, SC,
-                  [(x, x0 + a, x0 + a + n), (y, y0 + a, y0 + a + n), (off, c, c + n // 16)], [("X", 0, S[d])])
+    for d, n, x, x0, y, y0 in ((4, 256, "ca", 1536, "cb", 1536), (3, 512, "X", S[3], "u3", 0)):
+        for c in (0, 240):
+            c += (S[d] - 4096) // 16
+            V(lambda d=d, c=c, n=n, x=x, x0=x0, y=y, y0=y0: g.vector.tensor_tensor(
+                T.X[:, 0:S[d]].indirect(T.lr[:, c:c + n // 16]), T[x][:, x0:x0 + n], T[y][:, y0:y0 + n], OP.add), n, SC,
+              [(x, x0, x0 + n), (y, y0, y0 + n), ("lr", c, c + n // 16)], [("X", 0, S[d])])
         if d == 4:
             gate[0] = len(ops) - 1
-    n = K["DOWN"][2]
-    for a in range(0, 1024, n):
+    for a in (0, 512):
         skew[0] = a * K["SK"][1]
-        (single if (2, a) in K["DN_1"] else double)([("m1", "win", S[2] + a), ("i1", "X", S[2] + a)], n // 2, "X", 4096 + a, True, 0.0,
-                                                    [("ca", a), ("cb", a)], 128, K["E2"])
-        if a == K["G1"]:
-            first = len(ops) - 2
-    gate[0] = first
-    n = K["DOWN"][1]
-    for a in range(0, 1024, n):
-        for k, own in enumerate(("ca", "cb")):
-            skew[0] = (2 * a + k * n) * K["SK"][1]
-            (single if (1, a, k) in K["DN_1"] else double)([("m1", own, a), ("i1", "X", 4096 + a)], n // 2, "X", 2048 + 1024 * k + a, True, 0.0,
-                                                           [("s1", 1024 * k + a)], 0, K["E1"])
+        ps = double([("m1", "win", S[2] + a), ("i1", "X", S[2] + a)], 256, None, 0, True, early=3, short=128)
+        tt("sb", a, "cb", a, ps, 0, 512, 1, OP.add)
+        if a not in K["RIGHT"]:
+            tt("sb", 1024 + a, "ca", a, ps, 0, 512, 1, OP.add)
+        ps = newbank()
+        mm(ps, [("i1", "ca", a), ("i1", "sb", a)], 512)
+        out("X", 9984 + a, ps, 512)
+    for k, a in K["ORDER"]:
+        skew[0] = (2 * a + k * 512) * K["SK"][1]
+        terms = [("m1", "cb", a), ("i1", "X", 9984 + a)] if k and a in K["RIGHT"] else [("i1", "sb", 1024 * k + a)]
+        double(terms, 256, "X", S[5] + 1024 * k + a, True, 0.0, [("s1", 1024 * k + a)])
     skew[0], gate[0] = 0, len(ops) - 2
-    op("Y", [lambda: g.sync.dma_start(T.X[:, 5120:6144], T.X[:, 4096:5120])], 100, [("X", 4096, 5120)], [("X", 5120, 6144)], lat=2500, dma="dup", inc=16)
+    dma("Y", [(T.X[:, 11008:12032], T.X[:, 9984:11008])], [("X", 9984, 11008)], [("X", 11008, 12032)], 3000)
 
     def sel(d0, s0, src, pat, o, base, cm):
         G(lambda: g.affine_select(T.gsum[:, d0:d0 + 32], T[src][:, s0:s0 + 32], pat, o, 0.0, base, cm), 32, [reg(src, s0, 32)], [("gsum", d0, d0 + 32)])
 
-    fill("eight", 0, 128, 0, 32, 8.0)
     sel(160, 0, "eight", [[-16, 8], [0, 4]], OP.is_ge, 0, 1)
     sel(128, 160, "gsum", [[16, 8], [0, 4]], OP.is_ge, 15, -1)
     for b in range(4):
         sel(32 * b, 128, "gsum", [[0, 8], [1, 4]], OP.is_equal, -b, 0)
 
-    blocks, n, mid, mid2 = range(0, 2048, 512), 256, {}, {}
-    for a in blocks:
-        gather(on("i", a), "ine", a, "win", 0, S[5], "cu", 128 + a // 16, 512, -128.0)
+    mid, own, n = {}, 512 * rank, 256
+    for a in range(0, 2048, 512):
+        gather(on("i", a), "ine", (a + own) % 2048, "win", 0, S[5], "cu", 128 + (a + own) % 2048 // 16, 512, -128.0)
+    oles = []
 
-    def outer(a, n):
-        w, c = 2 * n, a // 16
-        if a in K["BY_V"]:
-            V(lambda: g.vector.tensor_tensor(T.ole[:, a:a + w], T.X[:, 2048:S[5]].indirect(T.e1[:, c:c + w // 16]), T.ine[:, a:a + w], OP.subtract), w, GA,
-              [("X", 2048, S[5]), ("e1", c, c + w // 16), ("ine", a, a + w)], [("ole", a, a + w)])
+    def clades():
+        back = others[::-1]
+        for k, q in enumerate(back + [rank]):
+            dst, off = ("land", "cu") if q == rank else ("clout", "cin")
+            gather(on("c", k), dst, 512 * q, "win", 0, S[5], off, 32 * q, 512, -128.0)
+            if k >= K["HELD"]:
+                ops[-1]["after"] = oles[K["AFTER"]]
+        for part in K["SENDS"]:
+            exchange("clout", "land", 512, "clr", K["BACK"], [back[k] for k in part], [others[k] for k in part])
+
+    def outer(a):
+        c, by_v = a // 16, (a - own) % 2048 in K["BY_V"]
+        if by_v:
+            V(lambda: g.vector.tensor_tensor(T.ole[:, a:a + 512], T.X[:, S[2]:12032].indirect(T.e1[:, c:c + 32]), T.ine[:, a:a + 512], OP.subtract), 512, GA,
+              [("X", S[2], 12032), ("e1", c, c + 32), ("ine", a, a + 512)], [("ole", a, a + 512)])
         else:
-            gather("A", "ole", a, "X", 2048, S[5], "e1", c, w)
-        terms = ([] if a in K["BY_V"] else [("m1", "ine", a)]) + [("i1", "ole", a)]
-        double(terms, n, "s2", a, True, 0.0, [("ine", a)], 0, 0 if a in K["BY_V"] else K["E0"])
+            gather("A", "ole", a, "X", S[2], 12032, "e1", c, 512)
+        oles.append(len(ops) - 1)
+        terms = ([] if by_v else [("m1", "ine", a)]) + [("i1", "ole", a)]
+        double(terms, n, "s2", a, True, 0.0, [("ine", a)], 0 if by_v else K["E0"])
 
-    def edge(a, n):
-        mid2[a] = split([("i1", "s2", a)], n, "pure")
+    def edge(a):
+        mid[a] = split([("i1", "s2", a)], n, "pure")
 
-    def test(a, n):
-        o = split([("i1", "s2", a), ("i1", "land", a)], n, "test", mid2[a], a)
+    def test(a):
+        o = split([("i1", "s2", a), ("i1", "land", a)], n, "test", mid[a], a)
         act("zz", a + n, "tt", 2 * o + n, n, AF.Relu, -2.0 ** -PB, 1.0)
         ps = newbank()
         fns = []
-        for kk in range(n // 128):
+        for kk in (0, 1):
             k = a // 256 + kk
             for b in range(4):
                 fns.append(lambda kk=kk, b=b: g.tensor.matmul(
@@ -418,28 +400,33 @@ def rank_program(g, core, T, topo):
             fns.append(lambda kk=kk, k=k: g.tensor.matmul(
                 B[ps][0:32, 64 * kk:64 * kk + 64], T.kmat[:, 32 * k:32 * k + 32], T.inv[:], False, True))
         P(fns, 64, [("gsum", 0, 128), ("zz", a, a + 2 * n), ("kmat", 0, 256), ("inv", 0, 64)], [(ps, 0, 512)])
-        for kk in range(n // 128):
-            k = a // 256 + kk
-            if k == 0:
-                A(lambda: g.scalar.activation(T.key[:, 0:64], B[ps][0:32, 0:64], AF.Copy), 64, 1, [(ps, 0, 512)], [("key", 0, 64)])
-            else:
-                dst, r = ("key", 64 * k) if k < 7 else ("keyi", 0)
-                V(lambda kk=kk, k=k, dst=dst, r=r: g.vector.tensor_tensor(T[dst][:, r:r + 64], T.key[:, 64 * k - 64:64 * k], B[ps][0:32, 64 * kk:64 * kk + 64], OP.min),
-                  64, 1, [(ps, 0, 512), ("key", 64 * k - 64, 64 * k)], [(dst, r, r + 64)])
 
-    parts = [(sum(K["PARTS"][:k]), w // 2) for k, w in enumerate(K["PARTS"])]
-    for step in range(len(parts) + 2):
-        for k, stage in reversed(list(enumerate((outer, edge, test)))):
-            if 0 <= step - k < len(parts):
-                skew[0] = parts[step - k][0] * K["SK"][2]
-                stage(*parts[step - k])
-    skew[0] = 0
-    ts("keyi", 64, "keyi", 0, 64, 1, 3, OP.logical_shift_right)
-    ts("keyi", 128, "keyi", 0, 64, 1, 7, OP.bitwise_and)
-    ts("res", 0, "keyi", 64, 64, 1)
-    ts("res", 64, "keyi", 128, 64, 1)
-    op("Y", [lambda: g.sync.dma_start(T.cost[:], T.res[:, 0:64])], 120, [("res", 0, 64)], [], lat=2000, dma="ld10", inc=16)
-    op("A", [lambda: g.scalar.dma_start(T["first"][:], T.res[:, 64:128])], 120, [("res", 64, 128)], [], lat=2000, dma="ld11", inc=16)
+        def least(dst, r, x, c, w):
+            V(lambda: g.vector.tensor_tensor(T[dst][:, r:r + w], T.key[:, x:x + w], B[ps][0:32, c:c + w], OP.min), w, 1, [(ps, 0, 512), ("key", x, x + w)], [(dst, r, r + w)])
+
+        r = (a - own) % 2048 // 4
+        if r == 0 and on("key", 0) == "A":
+            act("key", 0, ps, 0, 128, p=32)
+        elif r == 0:
+            ts("key", 0, ps, 0, 128, 1, p=32)
+        elif r < 384:
+            least("key", r, r - 128, 0, 128)
+        else:
+            tt("key", 384, "key", 256, "key", 320, 64, 2, OP.min)
+            least("key", 448, 384, 0, 64)
+            least("keyi", 0, 448, 64, 64)
+
+    for stage in (outer, edge, test):
+        for a in range(0, 2048, 512):
+            stage((a + own) % 2048)
+        if stage == outer:
+            clades()
+    ts("keyi", 64, "keyi", 0, 64, 1, 3, OP.logical_shift_right, p=32)
+    ts("keyi", 128, "keyi", 0, 64, 1, 7, OP.bitwise_and, p=32)
+    ts("res", 0, "keyi", 64, 64, 1, p=32)
+    ts("res", 64, "keyi", 128, 64, 1, p=32)
+    dma("Y", [(T.cost[:], T.res[:, 0:64])], [("res", 0, 64)], [], 2000)
+    dma("A", [(T["first"][:], T.res[:, 64:128])], [("res", 64, 128)], [], 2000)
 
     run(g, T, ops, B, hold)
 
@@ -460,7 +447,7 @@ def run(g, T, ops, B, hold):
                     same = ops[j]["eng"] == o["eng"]
                     if not w and kind == "R" and (same or not psum):
                         continue
-                    hard = (w and kind == "R") or not same or ops[j]["dma"] is not None or (o["eng"] != "P" and K["WAW"])
+                    hard = (w and kind == "R") or not same or ops[j]["dma"] is not None or o["eng"] != "P"
                     deps[i][j] = deps[i].get(j, False) or hard
         for r in o["R"]:
             hist.setdefault(r[0], []).append((r[1], r[2], i, False))
@@ -548,7 +535,7 @@ def run(g, T, ops, B, hold):
             if eng[i]:
                 free[eng[i]] = t
             fin[i] = t + lat[i] * (2 if k == 2 else 1)
-        return max(fin) * (.8, 1.1, .9)[k]
+        return max(fin) * (.8, 1.1, .5)[k]
 
     def backward(fin):
         free, back = {None: 0.0}, [0.0] * n
@@ -582,9 +569,9 @@ def run(g, T, ops, B, hold):
             plan = forward(tail)
             plans.append((plan[0], rnd, plan, tail))
             back = backward(plan[2])
-            tail = [back[i] - (ops[i]["late"] if ops[i]["late"] < K["CUT"] else 0) for i in range(n)]
+            tail = [back[i] - min(ops[i]["late"], 0) for i in range(n)]
         plan, tail = min(plans)[2:]
-        pairs, rnd = [], 0
+        rnd = 0
         while rnd < K["MORE"]:
             end, order, fin, place, before = plan
             prev, last, pairs = {}, {}, []
@@ -603,14 +590,13 @@ def run(g, T, ops, B, hold):
                 i, j = pairs[(7 * rnd + 3) % len(pairs)]
                 rnd += 1
                 new = list(tail)
-                new[i], new[j] = max(tail[i], tail[j]) + K["UP"], min(tail[i], tail[j]) - K["UP"] * (rnd % 3)
+                new[i], new[j] = max(tail[i], tail[j]) + K["UP1"], min(tail[i], tail[j]) - K["UP1"] * (rnd % 3)
                 other = forward(new)
-                if other[0] <= plan[0] + K["TOL"] and other[1] != plan[1]:
+                if other[0] <= plan[0] and other[1] != plan[1]:
                     plan, tail = other, new
-                    plans.append((plan[0], K["ROUNDS"] + rnd, plan))
                     break
-        PLAN["plan"] = min(plans)[2]
-        PLAN["all"] = [int(p[0]) for p in plans[:5]] + [len(plans), int(min(plans)[0])]
+        PLAN["plan"] = plan
+        PLAN["all"] = [int(max(plan[2]))]
     end, order, fin, place, before = PLAN["plan"]
     for b in place:
         B[b] = T[place[b]]
@@ -652,4 +638,3 @@ def run(g, T, ops, B, hold):
     for s in sorted(total):
         if clock["Y"].get(s, 0) < total[s]:
             g.sync.wait_ge(T.sem[s], total[s])
-    return fin

from concourse.bass import DstId, RemoteDMATransfer
from concourse.mybir import AluOpType as OP, ActivationFunctionType as AF

S = [0, 4096, 6144, 7168, 7680, 7936]
NT = 28
PB = 16
K = {
    "CONV": (256,) * 8, "CONV_A": (512, 1536),
    "UP": {1: 512, 2: 256, 3: 256, 4: 256},
    "UP_A": (), "BY_V": (0, 1536), "WCH": 256, "WLR": (512, 512), "E0": 3, "HELD": 3, "AFTER": 1, "SENDS": ((0, 1, 2),),
    "ON_V": tuple(("r", a) for a in (0, 512, 1024, 2048, 2304, 2560, 2816, 3072, 3328, 3584)) + (("s", 0), ("s", 512), ("X", 8448), ("X", 9472)),
    "LOADS": (("Y", "leaf", (0, 1024)), ("A", "left", 0), ("A", "right", 0), ("Y", "leaf", (1024, 1024)),
              ("Y", "leaf", (2048, 1024)), ("Y", "leaf", (3072, 1024)), ("A", "clade", 0), ("Y", "edge", 0)),
    "FIX": (30, 140, 70), "GA": 1.4, "SC": 3.2, "PE": .35, "HOP": 180, "OWN": 180, "T0": 1500, "DT": 350, "DMA": 2300,
    "SK": (1, 2), "EARLY": 30000, "FIRST": 45000, "TOP": 3000, "FP": (8, 6), "RIGHT": (), "ORDER": ((0, 0), (1, 0), (0, 512), (1, 512)), "FEED": 300, "CSK": .5, "CONST": 0, "TURN": 3500, "BACK": 5000,
    "WIN": 60, "KEEP": 1, "DEEP": 4, "LOOK": 2, "URG": 1000, "FR": .8, "ROUNDS": 5, "MORE": 120, "UP1": 100, "ROB": 1, "TRIES": 0, "HOT": 80,
}
K.update(CONV_A=(512,), RIGHT=(512,), GA=1.55, SC=3.8, FEED=0, FR=.9, MORE=100, ROB=2, ON_V=K["ON_V"] + (("s", 1536), ("r", 1536)))
PLAN = {}

BUFS = {
    "bfloat16": {"raw": 2048, "win": 7936, "X": 12032, "Y": 6144, "ca": 1792, "cb": 1792, "u3": 512, "sb": 2048, "tt": 512 * NT, "s1": 2048, "s2": 2048,
                 "ole": 2048, "ine": 2048, "zz": 2048, "land": 2048, "clout": 2048, "one": 512, "gsum": 192, "eight": 32,
                 "kc": 128, "ke": 128, "kmat": 256, "inv": 64},
    "float32": {"key": 512, "res": 128, "W": 7936, "val": 2048, "ek": 256, "el": 128, "i1f": 128, "ef": 128},
    "int32": {"ej": 128, "tS": 256 * NT, "tT": 256 * NT, "li": 480, "ci": 256, "keyi": 192},
    "uint16": {"lr": 480, "cu": 256, "cin": 128, "e1": 128, "ev": 128},
}
DIAG = {"i1": 1.0, "m1": -1.0, "iq": 2.0 ** PB, "mq": -2.0 ** PB, "ip": 2.0 ** -PB, "i14": 2.0 ** 14, "ik": -256.0, "kn": -2.0 ** 33, "kp": 2.0 ** 33,
        "i33": 33.0, "h33": 33.0 * 2 ** 14, "i16": 16.0, "f2": -31.0, "f4": 62.0, "f8": -124.0}
SCRATCH = {}
for _t in BUFS:
    for _b in BUFS[_t]:
        SCRATCH[_b] = ("sbuf", [32 if _b in ("key", "keyi", "res") else 128, BUFS[_t][_b]], _t)
for _b in DIAG:
    SCRATCH[_b] = ("sbuf", [128, 128], "bfloat16")
for _b in range(8):
    SCRATCH["pb%d" % _b] = ("psum", [128, 512], "float32")
SEMAPHORES = (["qV", "qA", "qP", "qG", "snd"] + ["d%d" % i for i in range(32)] + ["lst%d" % i for i in range(4)] + ["clr%d" % i for i in range(4)])


def rank_program(g, core, T, topo):
    rank = T.rank_of(core)
    if rank is None:
        return
    others = [(rank + k) % len(T.cores) for k in range(1, len(T.cores))]
    ops, hold, skew, gate = [], {}, [0], [None]
    B = dict((b, T[b]) for b in SCRATCH)
    GA, SC = K["GA"], K["SC"]
    RANGE = ({GA: 1.95, SC: 5.3}, {GA: 1.1, SC: 1.9})
    bank, slots, sems = [0], [0], [0]

    def op(eng, fns, cost, R=(), W=(), lat=0.0, dma=None, inc=0, seen=None):
        ops.append({"eng": eng, "fns": fns, "cost": cost, "R": list(R), "W": list(W), "lat": lat, "dma": dma, "inc": inc, "seen": seen,
                    "late": skew[0]})

    def V(fn, n, c, R, W):
        op("V", [fn], K["FIX"][0] + .83 * max(64, n * c), R, W)
        ops[-1]["more"] = [.83 * n * (x.get(c, c) - c) for x in RANGE]

    def A(fn, n, c, R, W):
        op("A", [fn], K["FIX"][1 if c == 1 else 2] + .83 * n * c, R, W)
        ops[-1]["more"] = [.83 * n * (x.get(c, c) - c) for x in RANGE]

    def P(fns, n, R, W):
        op("P", fns, K["FP"][0] + (K["FP"][1] + K["PE"] * max(64, n)) * len(fns), R, W)

    def G(fn, n, R, W):
        op("G", [fn], 150 + 1.66 * n, R, W)

    def dma(eng, pairs, R, W, lat=None, add=False):
        q = {"Y": g.sync, "A": g.scalar, "G": g}[eng]
        fns = [lambda o=o, i=i: g.dma_start(o, i, accum_op=OP.add) if add else q.dma_start(o, i) for o, i in pairs]
        op(eng, fns, (1100 if eng == "G" else 100) * len(pairs), R, W, lat=lat or K["DMA"], dma="d%d" % sems[0], inc=16)
        sems[0] += 1

    on = lambda k, a: "V" if (k, a) in K["ON_V"] else "A"

    def newbank(held=0):
        bank[0] += 1
        hold["ps%d" % bank[0]] = (0, K["KEEP"], K["DEEP"])[held]
        return "ps%d" % bank[0]

    def newslot(n):
        a = slots[0] if slots[0] % (256 * NT) + n <= 256 * NT else slots[0] + 256
        slots[0] = a + n
        return a % (256 * NT)

    def reg(b, a, n):
        return (b, 0, 512) if b[:2] == "ps" else (b, a, a + n)

    def mm(ps, terms, n, start=True, stop=True):
        fns = []
        for k, (m, b, a) in enumerate(terms):
            st, sp = start and k == 0, stop and k == len(terms) - 1
            fns.append(lambda m=m, b=b, a=a, st=st, sp=sp: g.tensor.matmul(B[ps][:, 0:n], T[m][:, 0:128], T[b][:, a:a + n], st, sp))
        P(fns, n, [(m, 0, 128) for m, b, a in terms] + [(b, a, a + n) for m, b, a in terms], [(ps, 0, 512)])

    def ts(dst, d0, src, s0, n, c, s1=None, op0=None, s2=None, op1=None, p=128):
        o, i = (lambda: B[dst][0:p, d0:d0 + n]), (lambda: B[src][0:p, s0:s0 + n])
        if op0 is None:
            fn = lambda: g.vector.tensor_copy(o(), i())
        elif op1 is None:
            fn = lambda: g.vector.tensor_scalar(o(), i(), s1, None, op0)
        else:
            fn = lambda: g.vector.tensor_scalar(o(), i(), s1, s2, op0, op1)
        V(fn, n, c, [reg(src, s0, n)], [reg(dst, d0, n)])

    def tt(dst, d0, x, x0, y, y0, n, c, o):
        V(lambda: g.vector.tensor_tensor(B[dst][:, d0:d0 + n], B[x][:, x0:x0 + n], B[y][:, y0:y0 + n], o), n, c,
          [reg(x, x0, n), reg(y, y0, n)], [reg(dst, d0, n)])

    def act(dst, d0, src, s0, n, func=AF.Copy, scale=1.0, bias=0.0, p=128):
        A(lambda: g.scalar.activation(B[dst][0:p, d0:d0 + n], B[src][0:p, s0:s0 + n], func, bias=bias, scale=scale), n, 1,
          [reg(src, s0, n)], [reg(dst, d0, n)])

    def out(dst, d0, src, n, bias=0.0, s0=0):
        if on(dst, d0) == "V":
            ts(dst, d0, src, s0, n, 1, *((bias, OP.add) if bias else ()))
        else:
            act(dst, d0, src, s0, n, AF.Copy, 1.0, bias)

    def fill(buf, p0, p1, a, b, x):
        V(lambda: g.vector.memset(T[buf][p0:p1, a:b], x), b - a, .5, [], [(buf, a, b)])

    def turn(src, c0, rows, cols):
        ps = newbank()
        P([lambda: g.tensor.transpose(B[ps][0:cols, 0:rows], T[src][0:rows, c0:c0 + cols], T.i1f[0:rows, 0:rows])], 512,
          [(src, c0, c0 + cols), ("i1f", 0, 128)], [(ps, 0, 512)])
        return ps

    HIGH = {"i1": "iq", "m1": "mq"}

    def split(terms, n, kind, add=None, z=None, early=0, short=0):
        pp, o, pb = newbank(2 * (early & 1) if add is None else 1), newslot(max(n, 256)), 14 if kind == "edge" else PB
        both = [x for m, b, a in terms for x in (("i14" if kind == "edge" else HIGH[m], b, a + n), (m, b, a))]
        if add is not None:
            mm(pp, both[:1], n, stop=False)
            both = [("kn", "tt", 2 * add + n), ("kp", "tt", 2 * add + n), both[1], ("kn", "tt", 2 * add), ("kp", "tt", 2 * add)] + both[2:]
        if early & 1:
            mm(pp, both[:2], n, stop=False)
            ops[-1]["after"] = gate[0]
        mm(pp, both[2 * (early & 1):], n, start=not early & 1 and add is None)
        ops[-1]["late"] = min(skew[0], 0) - K["FEED"]
        short += 256 if kind == "edge" else 0
        if add is not None:
            tt("tS", o, "tT", add, pp, 0, n, 1, OP.add)
        else:
            ts("tS", o, pp, 0, n, 1, *((float((short << pb) + short), OP.add) if short else ()))
        top = 0xD5 if kind == "edge" else 0x55
        ts("tT", o, "tS", o, n, 1, 1, OP.logical_shift_right, top + (top << pb), OP.bitwise_and)
        if kind == "edge":
            ts("tt", 2 * o + n, "tT", o, n, 1, 2.0 ** -pb, OP.mult)
        else:
            ts("tt", 2 * o + n, "tT", o, n, 1, 1.5 * 2.0 ** (23 + pb), OP.add, 1.5 * 2.0 ** (23 + pb), OP.subtract)
        mm(pp, [("i14" if kind == "edge" else "i1", "tt", 2 * o + n)], n)
        ops[-1]["late"] = min(skew[0], 0) - K["FEED"]
        if kind == "test":
            tt("zz", z, "tT", o, pp, 0, n, 1, OP.is_equal)
        else:
            tt("tt", 2 * o, "tT", o, pp, 0, n, 1, OP.subtract)
        return o

    def absorb(ps, o, n, more=()):
        mm(ps, [("kn", "tt", 2 * o), ("kp", "tt", 2 * o)] + [("i1", b, a) for b, a in more], 2 * n, start=False, stop=False)
        P([lambda: g.tensor.matmul(B[ps][:, 0:n], T.i1[:], T.tt[:, 2 * o:2 * o + n], False, False),
           lambda: g.tensor.matmul(B[ps][:, n:2 * n], T.ip[:], T.tt[:, 2 * o + n:2 * o + 2 * n], False, True)], n,
          [("i1", 0, 128), ("ip", 0, 128), ("tt", 2 * o, 2 * o + 2 * n)], [(ps, 0, 512)])

    def double(terms, n, dst, d0, plain, bias=128.0, more=(), early=0, short=0):
        o, ps = split(terms, n, "pure" if plain else "edge", early=early, short=short), newbank(2 if early & 2 else 1)
        terms = ([("one", "one", 0)] if short else []) + ([] if plain else [("ke", "one", 0)]) + terms
        if early & 2:
            mm(ps, terms[:-1], 2 * n, stop=False)
            ops[-1]["after"] = gate[0]
        mm(ps, terms[-1:] if early & 2 else terms, 2 * n, start=not early & 2, stop=False)
        if not plain:
            mm(ps, [("ik", "tt", 2 * o)], 2 * n, start=False)
            tt(dst, d0, "tt", 2 * o, ps, 0, 2 * n, 1, OP.max)
        elif dst is None:
            absorb(ps, o, n)
        elif more and on(dst, d0) == "V":
            absorb(ps, o, n, more[1:])
            tt(dst, d0, *more[0], ps, 0, 2 * n, 1, OP.add)
        else:
            absorb(ps, o, n, more)
            out(dst, d0, ps, 2 * n, bias)
        return ps

    def gather(eng, dst, d0, src, a, b, off, c0, n, bias=0.0):
        ind = lambda: T[src][:, a:b].indirect(T[off][:, c0:c0 + n // 16])
        R, W = [(src, a, b), (off, c0, c0 + n // 16)], [(dst, d0, d0 + n)]
        if eng == "V" and bias:
            V(lambda: g.vector.tensor_scalar(T[dst][:, d0:d0 + n], ind(), bias, None, OP.add), n, GA, R, W)
        elif eng == "V":
            V(lambda: g.vector.tensor_copy(T[dst][:, d0:d0 + n], ind()), n, GA, R, W)
        else:
            A(lambda: g.scalar.activation(T[dst][:, d0:d0 + n], ind(), AF.Copy, bias=bias), n, GA, R, W)

    def scatter(b, c0, src, s0, n):
        to, R = (lambda: T.W[:, 0:b].indirect(T.lr[:, c0:c0 + n // 16])), [(src, s0, s0 + n), ("lr", c0, c0 + n // 16)]
        if on("q", c0) == "V":
            V(lambda: g.vector.tensor_copy(to(), T[src][:, s0:s0 + n]), n, SC, R, [("W", 0, b)])
        else:
            A(lambda: g.scalar.activation(to(), T[src][:, s0:s0 + n], AF.Silu), n, SC, R, [("W", 0, b)])

    SRC = {"leaf": ("raw", 1024, 0), "left": ("li", 240, 0), "right": ("li", 240, 240), "clade": ("ci", 128, 0), "edge": ("ci", 128, 128)}
    for i, (eng, src, a) in enumerate(K["LOADS"]):
        dst, w, d0 = SRC[src]
        if src == "leaf":
            a, w = a
            dst, d0 = ("Y", a) if a < 2048 else ("raw", a - 2048)
        skew[0] = -1e6 + 1e4 * i
        dma(eng, [(T[dst][:, d0:d0 + w], T[src][:, a:a + w])], [], [(dst, d0, d0 + w)], K["T0"] + K["DT"] * i + {"clade": 1500, "edge": 6000}.get(src, 0))
    skew[0] = -9e5
    dma("Y", [(T.ej[:, 16 * q:16 * q + 16], T.edge[16 * q:16 * q + 16, :]) for q in range(8)], [], [("ej", 0, 128)], 16000)
    skew[0] = -K["CONST"]

    fill("one", 0, 128, 0, 512, 1.0)
    G(lambda: g.affine_select(T.i1[:], T.one[:, 0:128], [[-1, 128]], OP.is_equal, 0.0, 0, 1), 128, [("one", 0, 128)], [("i1", 0, 128)])
    for nm in DIAG:
        if nm != "i1":
            ts(nm, 0, "i1", 0, 128, .5, DIAG[nm], OP.mult)
    ts("i1f", 0, "i1", 0, 128, 1)
    fill("ke", 0, 64, 0, 128, 512.0)
    fill("ke", 64, 128, 0, 128, 2.0)
    fill("kc", 0, 64, 0, 128, -2.0 ** 15)
    fill("kc", 64, 128, 0, 128, -2.0)
    fill("inv", 0, 128, 0, 64, 2.0 ** -7)
    fill("eight", 0, 128, 0, 32, 8.0)
    skew[0] = 0

    def ramp(buf, a, n, step, base):
        G(lambda: g.iota(T[buf][:, a:a + n], [[step, n]], base, 0, allow_small_or_imprecise_dtypes=True), n, [("i1", 0, 128)], [(buf, a, a + n)])

    for a in range(0, 2048, 512):
        ramp("val", a, 512, 1, 4096 + a)
    ramp("W", S[2], S[5] - S[2], 1, 4096 - 1792)
    G(lambda: g.iota(T.kmat[:], [[1, 8], [0, 32]], 0, 0, allow_small_or_imprecise_dtypes=True), 256, [], [("kmat", 0, 256)])

    ts("cu", 128, "ci", 128, 128, 1)
    skew[0] = -K["EARLY"]
    ts("lr", 0, "li", 0, 480, 1)
    skew[0] = -K["FIRST"]
    ts("cu", 0, "ci", 0, 128, 1)

    def fused(src, dst, w, sem, whom):
        tr = []
        for q in whom:
            i, to = others.index(q), T.cores[q]
            rid, pid, _e = topo.addr(to)
            en = topo.engines(core, to)[4 * i:4 * i + 4]
            tr.append(RemoteDMATransfer(dst_ids=[DstId(rid=rid, pnc=pid)], dma_engine_mask=sum(1 << e for e in en),
                                        remote_sem=T.sem[sem + str(rank)], src=T[src][:, w * q:w * q + w],
                                        dst=T[dst][:, w * rank:w * rank + w]))
        g.remote_dma_fused(tr, local_sem=T.sem.snd)

    def exchange(src, dst, w, sem, t, whom, whence):
        op("G", [lambda: fused(src, dst, w, sem, whom)], 1500, [(src, w * q, w * q + w) for q in whom], [], lat=2000, dma="snd", inc=4 * len(whom))
        me = len(ops) - 1
        for q in whence:
            op(None, [], t, [], [(dst, w * q, w * q + w)], seen=(sem + str(q), 4))
            ops[-1]["after"] = me

    exchange("cu", "cin", 32, "lst", 9000, others, others)

    skew[0] = 0

    for k, n in enumerate(K["CONV"]):
        a, pp = 2 * sum(K["CONV"][:k]), newbank()
        raw, r = ("Y", a) if a < 2048 else ("raw", a - 2048)
        skew[0] = (a // 1024 * 1024 - 4096) * K["CSK"]
        if a in K["CONV_A"]:
            f = ("sb", "s2", "ole", "zz")[k % 4]
            ts(f, 0, raw, r, 512, .5, .5, OP.mult, 132 - .25, OP.add)
            ts(f, 512, raw, r, 512, .5, .25, OP.mult, 131 - .375, OP.add)
            ts(f, 1024, raw, r, 512, .5, 8.0, OP.is_ge, -37.0, OP.add)
            mm(pp, [("f2", f, 0), ("f4", f, 512), ("f8", f, 1024), ("i16", raw, r)], 512)
            act("win", a, pp, 0, 512, AF.Copy, 1.0, 128.0 + 31 * 132 - 62 * 131 - 124 * 37)
            continue
        o = newslot(n)
        mm(pp, [("h33", raw, r + n), ("i33", raw, r)], n)
        ts("tS", o, pp, 0, n, 1)
        ts("tT", o, "tS", o, n, 1, 1, OP.logical_shift_right, 0x55 + (0x55 << 14), OP.bitwise_and)
        ts("win", a + n, "tT", o, n, 1, 2.0 ** -14, OP.mult, 128.0, OP.add)
        mm(pp, [("kc", "one", 0), ("i14", "win", a + n)], n)
        tt("win", a, "tT", o, pp, 0, n, 1, OP.subtract)

    skew[0] = 0
    place = lambda a: 240 * (a // 1024) + 128 + a % 1024 // 16
    for a in range(0, 2048, K["WCH"]):
        scatter(S[2], place(a), "val", a, K["WCH"])
    for k, w in enumerate(K["WLR"]):
        for a in range(0, 2048, w):
            scatter(S[1], 240 * k + a // 16, "W", S[1] + a, w)
    ts("ef", 0, "ej", 0, 128, 1)
    ts("ev", 0, turn("ef", 0, 128, 128), 0, 128, 1)

    CA = lambda c: ("Y", 2048 + c) if c < 2048 else ("ca", c - 2048)
    CB = lambda c: ("Y", 4096 + c) if c < 2048 else ("cb", c - 2048)
    for d in range(1, 5):
        n = K["UP"][d]
        for a in range(0, S[d + 1] - S[d], n):
            c = S[d] - 4096 + a
            skew[0] = a * K["SK"][0] if d < 4 else -K["TOP"]
            gather(on("l", c), *CA(c), "win", 0, S[d], "lr", c // 16, n, -128.0)
            gather(on("r", c), *CB(c), "win", 0, S[d], "lr", 240 + c // 16, n, -128.0)
            double([("i1", *CA(c)), ("i1", *CB(c))], n // 2, "win", S[d] + a, c in K["UP_A"])
    skew[0] = 0
    ts("X", S[4], "win", S[4], 256, .5, 85.0 - 128.0, OP.add)
    dma("G", [(T.Y[:, 4096:6144], T.Y[:, 2048:4096])], [("Y", 2048, 6144)], [("Y", 4096, 6144)], 11000, True)
    for a in range(0, 2048, 512):
        gather(on("s", a), "s1", a, "Y", 0, 6144, "lr", place(a), 512)
    ps = newbank()
    mm(ps, [("i1", "ca", 1024), ("i1", "cb", 1024), ("m1", "win", S[3])], 512)
    out("u3", 0, ps, 512, 128.0)

    for a in range(0, 2048, 512):
        gather(on("w", a), "val", a, "W", 0, S[5], "ev", a // 16, 512)
    for k, x in enumerate((2048.0, -2048.0)):
        ts("ek", 128 * k, "ci", 128, 128, 1, S[k + 1] - .5, OP.is_ge, x, OP.mult)
    tt("el", 0, "ek", 0, "ek", 128, 128, 2, OP.add)
    dma("G", [(T.el[:], T.val[0:128:16, :])], [("val", 0, 2048), ("el", 0, 128)], [("el", 0, 128)], K["TURN"], True)
    skew[0] = -K["TOP"]
    ts("e1", 0, "el", 0, 128, 1, 1792 - 4095.75, OP.add)
    skew[0] = 0

    for d, n, x, x0, y, y0 in ((4, 256, "ca", 1536, "cb", 1536), (3, 512, "X", S[3], "u3", 0)):
        for c in (0, 240):
            c += (S[d] - 4096) // 16
            V(lambda d=d, c=c, n=n, x=x, x0=x0, y=y, y0=y0: g.vector.tensor_tensor(
                T.X[:, 0:S[d]].indirect(T.lr[:, c:c + n // 16]), T[x][:, x0:x0 + n], T[y][:, y0:y0 + n], OP.add), n, SC,
              [(x, x0, x0 + n), (y, y0, y0 + n), ("lr", c, c + n // 16)], [("X", 0, S[d])])
        if d == 4:
            gate[0] = len(ops) - 1
    for a in (0, 512):
        skew[0] = a * K["SK"][1]
        ps = double([("m1", "win", S[2] + a), ("i1", "X", S[2] + a)], 256, None, 0, True, early=3, short=128)
        tt("sb", a, "cb", a, ps, 0, 512, 1, OP.add)
        if a not in K["RIGHT"]:
            tt("sb", 1024 + a, "ca", a, ps, 0, 512, 1, OP.add)
        ps = newbank()
        mm(ps, [("i1", "ca", a), ("i1", "sb", a)], 512)
        out("X", 9984 + a, ps, 512)
    for k, a in K["ORDER"]:
        skew[0] = (2 * a + k * 512) * K["SK"][1]
        terms = [("m1", "cb", a), ("i1", "X", 9984 + a)] if k and a in K["RIGHT"] else [("i1", "sb", 1024 * k + a)]
        double(terms, 256, "X", S[5] + 1024 * k + a, True, 0.0, [("s1", 1024 * k + a)])
    skew[0], gate[0] = 0, len(ops) - 2
    dma("Y", [(T.X[:, 11008:12032], T.X[:, 9984:11008])], [("X", 9984, 11008)], [("X", 11008, 12032)], 3000)

    def sel(d0, s0, src, pat, o, base, cm):
        G(lambda: g.affine_select(T.gsum[:, d0:d0 + 32], T[src][:, s0:s0 + 32], pat, o, 0.0, base, cm), 32, [reg(src, s0, 32)], [("gsum", d0, d0 + 32)])

    sel(160, 0, "eight", [[-16, 8], [0, 4]], OP.is_ge, 0, 1)
    sel(128, 160, "gsum", [[16, 8], [0, 4]], OP.is_ge, 15, -1)
    for b in range(4):
        sel(32 * b, 128, "gsum", [[0, 8], [1, 4]], OP.is_equal, -b, 0)

    mid, own, n = {}, 512 * rank, 256
    for a in range(0, 2048, 512):
        gather(on("i", a), "ine", (a + own) % 2048, "win", 0, S[5], "cu", 128 + (a + own) % 2048 // 16, 512, -128.0)
    oles = []

    def clades():
        back = others[::-1]
        for k, q in enumerate(back + [rank]):
            dst, off = ("land", "cu") if q == rank else ("clout", "cin")
            gather(on("c", k), dst, 512 * q, "win", 0, S[5], off, 32 * q, 512, -128.0)
            if k >= K["HELD"]:
                ops[-1]["after"] = oles[K["AFTER"]]
        for part in K["SENDS"]:
            exchange("clout", "land", 512, "clr", K["BACK"], [back[k] for k in part], [others[k] for k in part])

    def outer(a):
        c, by_v = a // 16, (a - own) % 2048 in K["BY_V"]
        if by_v:
            V(lambda: g.vector.tensor_tensor(T.ole[:, a:a + 512], T.X[:, S[2]:12032].indirect(T.e1[:, c:c + 32]), T.ine[:, a:a + 512], OP.subtract), 512, GA,
              [("X", S[2], 12032), ("e1", c, c + 32), ("ine", a, a + 512)], [("ole", a, a + 512)])
        else:
            gather("A", "ole", a, "X", S[2], 12032, "e1", c, 512)
        oles.append(len(ops) - 1)
        terms = ([] if by_v else [("m1", "ine", a)]) + [("i1", "ole", a)]
        double(terms, n, "s2", a, True, 0.0, [("ine", a)], 0 if by_v else K["E0"])

    def edge(a):
        mid[a] = split([("i1", "s2", a)], n, "pure")

    def test(a):
        o = split([("i1", "s2", a), ("i1", "land", a)], n, "test", mid[a], a)
        act("zz", a + n, "tt", 2 * o + n, n, AF.Relu, -2.0 ** -PB, 1.0)
        ps = newbank()
        fns = []
        for kk in (0, 1):
            k = a // 256 + kk
            for b in range(4):
                fns.append(lambda kk=kk, b=b: g.tensor.matmul(
                    B[ps][0:32, 64 * kk:64 * kk + 64], T.gsum[:, 32 * b:32 * b + 32],
                    T.zz[:, a + 256 * kk + 64 * b:a + 256 * kk + 64 * b + 64], b == 0, False))
            fns.append(lambda kk=kk, k=k: g.tensor.matmul(
                B[ps][0:32, 64 * kk:64 * kk + 64], T.kmat[:, 32 * k:32 * k + 32], T.inv[:], False, True))
        P(fns, 64, [("gsum", 0, 128), ("zz", a, a + 2 * n), ("kmat", 0, 256), ("inv", 0, 64)], [(ps, 0, 512)])

        def least(dst, r, x, c, w):
            V(lambda: g.vector.tensor_tensor(T[dst][:, r:r + w], T.key[:, x:x + w], B[ps][0:32, c:c + w], OP.min), w, 1, [(ps, 0, 512), ("key", x, x + w)], [(dst, r, r + w)])

        r = (a - own) % 2048 // 4
        if r == 0 and on("key", 0) == "A":
            act("key", 0, ps, 0, 128, p=32)
        elif r == 0:
            ts("key", 0, ps, 0, 128, 1, p=32)
        elif r < 384:
            least("key", r, r - 128, 0, 128)
        else:
            tt("key", 384, "key", 256, "key", 320, 64, 2, OP.min)
            least("key", 448, 384, 0, 64)
            least("keyi", 0, 448, 64, 64)

    for stage in (outer, edge, test):
        for a in range(0, 2048, 512):
            stage((a + own) % 2048)
        if stage == outer:
            clades()
    ts("keyi", 64, "keyi", 0, 64, 1, 3, OP.logical_shift_right, p=32)
    ts("keyi", 128, "keyi", 0, 64, 1, 7, OP.bitwise_and, p=32)
    ts("res", 0, "keyi", 64, 64, 1, p=32)
    ts("res", 64, "keyi", 128, 64, 1, p=32)
    dma("Y", [(T.cost[:], T.res[:, 0:64])], [("res", 0, 64)], [], 2000)
    dma("A", [(T["first"][:], T.res[:, 64:128])], [("res", 64, 128)], [], 2000)

    run(g, T, ops, B, hold)


def run(g, T, ops, B, hold):
    n, hop = len(ops), K["HOP"]
    deps = [dict() for _ in ops]
    hist = {}
    for i, o in enumerate(ops):
        if "after" in o:
            deps[i][o["after"]] = ops[o["after"]]["eng"] not in ("G", o["eng"])
        for kind, regs in (("R", o["R"]), ("W", o["W"])):
            for r in regs:
                psum = r[0][:2] == "ps"
                for (a, b, j, w) in hist.get(r[0], ()):
                    if j == i or not (a < r[2] and r[1] < b):
                        continue
                    same = ops[j]["eng"] == o["eng"]
                    if not w and kind == "R" and (same or not psum):
                        continue
                    hard = (w and kind == "R") or not same or ops[j]["dma"] is not None or o["eng"] != "P"
                    deps[i][j] = deps[i].get(j, False) or hard
        for r in o["R"]:
            hist.setdefault(r[0], []).append((r[1], r[2], i, False))
        for r in o["W"]:
            h = hist.get(r[0], [])
            hist[r[0]] = [e for e in h if not (r[1] <= e[0] and e[1] <= r[2])] + [(r[1], r[2], i, True)]
    succ = [[] for _ in ops]
    for i in range(n):
        for j in deps[i]:
            succ[j].append(i)
    cost, lat, eng = [o["cost"] for o in ops], [o["lat"] for o in ops], [o["eng"] for o in ops]
    users, bank = {}, [None] * n
    for i, o in enumerate(ops):
        for r in o["R"] + o["W"]:
            if r[0][:2] == "ps":
                bank[i] = r[0]
        if bank[i]:
            users.setdefault(bank[i], []).append(i)

    gap = lambda j, k: (K["OWN"] if eng[j] == eng[k] else hop) if deps[k][j] else 0

    def forward(tail):
        free, fin, order, done = {None: 0.0}, [0.0] * n, [], [False] * n
        need = [len(d) for d in deps]
        ready = [i for i in range(n) if not need[i]]
        est = dict((i, 0.0) for i in ready)
        left = dict((b, len(u)) for b, u in users.items())
        spare, place, before = [(0.0, "pb%d" % k, []) for k in range(8)], {}, {}
        todo = dict((e, [i for i in range(n) if eng[i] == e]) for e in set(eng))

        def start(i):
            t = max(est[i], free.get(eng[i], 0.0))
            if bank[i] and bank[i] not in place:
                if len(spare) <= hold[bank[i]]:
                    return 1e18
                t = max(t, min(spare)[0] + hop)
            return t

        def soon(i, depth):
            if i in est:
                return min(start(i), est[i] + 1000)
            if not depth:
                return 1e18
            return max(fin[j] if done[j] else soon(j, depth - 1) + cost[j] + lat[j] for j in deps[i]) + hop

        while ready:
            best = min(ready, key=start)
            e, bt = eng[best], start(best)
            if e:
                best = max([i for i in ready if eng[i] == e and start(i) <= bt + K["WIN"]], key=lambda i: (tail[i], -i))
                bt = start(best)
                if cost[best] > 300:
                    t = min([soon(i, K["LOOK"]) for i in todo[e] if tail[i] > tail[best] + K["URG"]] or [1e18])
                    if bt < t < bt + K["FR"] * cost[best]:
                        free[e] = t
                        continue
                free[e] = bt + cost[best]
            done[best], fin[best], b = True, bt + cost[best] + lat[best], bank[best]
            todo[e].remove(best)
            if b:
                if b not in place:
                    x = min(spare)
                    spare.remove(x)
                    place[b], before[best] = x[1], x[2]
                left[b] -= 1
                if not left[b]:
                    spare.append((max(fin[j] for j in users[b]), place[b], users[b]))
            order.append(best)
            ready.remove(best)
            for k in succ[best]:
                need[k] -= 1
                if not need[k]:
                    ready.append(k)
                    est[k] = max(fin[j] + gap(j, k) for j in deps[k])
        return max(fin) + K["ROB"] * sum(replay(order, before, k) for k in range(3)), order, fin, place, before

    def replay(order, before, k):
        free, fin = {}, [0.0] * n
        for i in order:
            t = max([free.get(eng[i], 0.0)] + [fin[j] + gap(j, i) for j in deps[i]] + [fin[j] + hop for j in before.get(i, ())])
            if k == 2:
                t += cost[i] * (1 if eng[i] else 2)
            else:
                t += cost[i] + ops[i].get("more", (0, 0))[k]
            if eng[i]:
                free[eng[i]] = t
            fin[i] = t + lat[i] * (2 if k == 2 else 1)
        return max(fin) * (.8, 1.1, .5)[k]

    def backward(fin):
        free, back = {None: 0.0}, [0.0] * n
        need = [len(x) for x in succ]
        ready = [i for i in range(n) if not need[i]]
        est = dict((i, lat[i]) for i in ready)
        start = lambda i: max(est[i], free.get(eng[i], 0.0))
        while ready:
            best = min(ready, key=start)
            e, bt = eng[best], start(best)
            if e:
                best = max([i for i in ready if eng[i] == e and start(i) <= bt + K["WIN"]], key=lambda i: (fin[i], i))
                bt = start(best)
                free[e] = bt + cost[best]
            back[best] = bt + cost[best]
            ready.remove(best)
            for k in deps[best]:
                need[k] -= 1
                if not need[k]:
                    ready.append(k)
                    est[k] = max(back[j] + gap(k, j) for j in succ[k]) + lat[k]
        return back

    if "plan" not in PLAN:
        tail = [0.0] * n
        for i in range(n - 1, -1, -1):
            tail[i] = cost[i] + lat[i] + max([tail[k] + hop for k in succ[i]] or [0.0])
        tail = [tail[i] - ops[i]["late"] for i in range(n)]
        plans = []
        for rnd in range(K["ROUNDS"]):
            plan = forward(tail)
            plans.append((plan[0], rnd, plan, tail))
            back = backward(plan[2])
            tail = [back[i] - min(ops[i]["late"], 0) for i in range(n)]
        plan, tail = min(plans)[2:]
        rnd = 0
        while rnd < K["MORE"]:
            end, order, fin, place, before = plan
            prev, last, pairs = {}, {}, []
            for i in order:
                prev[i], last[eng[i]] = last.get(eng[i]) if eng[i] else None, i
            i = max(order, key=lambda x: fin[x])
            while i is not None:
                t, j = fin[i] - cost[i] - lat[i], prev[i]
                near = max(list(deps[i]) + before.get(i, []) + [None], key=lambda x: -1e9 if x is None else fin[x])
                if j is not None and j not in deps[i] and (near is None or fin[near] + hop < t - 1):
                    pairs.append((i, j))
                    i = j
                else:
                    i = near
            for k in range(len(pairs)):
                i, j = pairs[(7 * rnd + 3) % len(pairs)]
                rnd += 1
                new = list(tail)
                new[i], new[j] = max(tail[i], tail[j]) + K["UP1"], min(tail[i], tail[j]) - K["UP1"] * (rnd % 3)
                other = forward(new)
                if other[0] <= plan[0] and other[1] != plan[1]:
                    plan, tail = other, new
                    break
        PLAN["plan"] = plan
        PLAN["all"] = [int(max(plan[2]))]
    end, order, fin, place, before = PLAN["plan"]
    for b in place:
        B[b] = T[place[b]]
    for i in before:
        for j in before[i]:
            deps[i][j] = deps[i].get(j, False) or eng[j] != eng[i]
    queue = {"V": g.vector, "A": g.scalar, "P": g.tensor, "G": g, "Y": g.sync}
    csem = {"V": "qV", "A": "qA", "P": "qP", "G": "qG"}
    total, val = {}, [None] * n
    clock = {e: {} for e in queue}
    snap = [None] * n
    for i in order:
        o = ops[i]
        e = o["eng"]
        if e is None:
            val[i], snap[i] = o["seen"], {}
            total[o["seen"][0]] = o["seen"][1]
            continue
        ck = clock[e]
        todo = sorted([j for j in deps[i] if deps[i][j]], key=lambda j: -fin[j])
        for j in todo:
            s = val[j][0]
            if ck.get(s, 0) >= val[j][1]:
                continue
            same = [x for x in todo if val[x][0] == s]
            v = max(val[x][1] for x in same)
            queue[e].wait_ge(T.sem[s], v)
            for x in same:
                for k2, v2 in snap[x].items():
                    ck[k2] = max(ck.get(k2, 0), v2)
            ck[s] = max(ck.get(s, 0), v)
        s = o["dma"] or csem[e]
        for fn in o["fns"]:
            ins = fn()
            if ins is not None:
                ins.then_inc(T.sem[s], o["inc"] or 1)
            total[s] = total.get(s, 0) + (o["inc"] or 1)
        val[i], snap[i] = (s, total[s]), dict(ck)
    for s in sorted(total):
        if clock["Y"].get(s, 0) < total[s]:
            g.sync.wait_ge(T.sem[s], total[s])
